import numpy as np, ml_dtypes
CORES = [3,11,19,27,35,43,51,59]
N = 8
BF = ml_dtypes.bfloat16
S, R, NF, PH, LB, RO = 1024, 8192, 512, 1024, 10, 3
def place(s, p):
    return ((s * p >> 4) + s + 37 * p) & (R - 1)
def records(rng):
    st = ((np.arange(8)[None, :] + rng.integers(0, 3, (N, 1))) % 3)[:, :, None, None]
    lo = np.where(st == 0, 0, np.where(st == 1, 64 * rng.integers(0, 4, (N, 8, 1, R)), 200 * (rng.random((N, 8, 1, R)) < 0.35))).astype(np.int32)
    span = np.where(st == 0, 256, np.where(st == 1, 64, 56)).astype(np.float32)
    x = np.minimum(lo + (rng.random((N, 8, 16, R), dtype=np.float32) * span).astype(np.int32), 255)
    u = rng.random((N, 8, 16, 1))
    th = np.where(st == 0, 1000 + 700 * u, np.where(st == 1, 256 + 2000 * u, 450 + 1150 * u)).astype(np.int64)
    return x, th
def parts(rng):
    var = rng.choice(np.array([0.2, 0.35, 0.5]), (N, 8, 1, 1)); emp = rng.choice(np.array([0.2, 0.45, 0.7]), (N, 8, 1, 1))
    tk = rng.integers(0, S, (N, 8, 16, S)) + S * (rng.random((N, 8, 16, S)) < var)
    fr = np.where(rng.random((N, 8, 16, NF)) < emp, -1, rng.integers(0, S * PH, (N, 8, 16, NF)))
    return tk, fr, rng.integers(0, S, (N, 8, NF)), rng.integers(0, NF, (N, 8, NF)), rng.integers(0, S, (N, 8, NF))
def pack(x, tk, fr, th, s, f, c):
    return {"x": np.ascontiguousarray(x.reshape(N, 128, R)).astype(np.float32).astype(BF), "sk": np.ascontiguousarray(tk.reshape(N, 128, S)).astype(np.int32),
            "fr": np.ascontiguousarray(fr.reshape(N, 128, NF)).astype(np.int32), "th": np.ascontiguousarray(th.reshape(N, 128, 1)).astype(np.int32),
            "gs": s.astype(np.int32), "gf": f.astype(np.int32), "gcl": c.astype(np.int32)}
def setup_inputs(rng):
    x, th = records(rng); tk, fr, s, f, c = parts(rng)
    return pack(x, tk, fr, th, s, f, c)
def setup_inputs_spread(rng):
    amp = np.exp2(8 * rng.random((N, 8, 1, R))).astype(np.float32)
    x = np.minimum((rng.random((N, 8, 16, R), dtype=np.float32) * amp).astype(np.int32), 255)
    x = np.where(rng.random((N, 8, 1, R)) < 0.0625, 255 - x, x)
    th = np.minimum(np.exp2(12 * rng.random((N, 8, 16, 1))).astype(np.int64), 4080)
    u = rng.random((N, 8, 16, S)); tk = np.minimum((2 * S * u * np.sqrt(u)).astype(np.int64), 2 * S - 1)
    v = rng.random((N, 8, 16, NF)); fr = np.where(rng.random(v.shape) < 0.3 * rng.random((N, 8, 1, 1)) + 0.1, -1, np.minimum((S * PH * v * v).astype(np.int64), S * PH - 1))
    w = rng.random((3, N, 8, NF)); w = w * w
    return pack(x, tk, fr, th, np.minimum((S * w[0]).astype(np.int64), S - 1), np.minimum((NF * w[1]).astype(np.int64), NF - 1), np.minimum((S * w[2]).astype(np.int64), S - 1))
def setup_inputs_ends(rng):
    one = rng.random((N, 8, 1, R)) < 0.5; each = rng.random((N, 8, 16, R)) < 0.5
    x = 255 * np.where(rng.random((N, 8, 1, R)) < 0.25, each, one).astype(np.int64)
    tk = (2 * S - 1) * rng.integers(0, 2, (N, 8, 16, S)); fr = np.where(rng.integers(0, 2, (N, 8, 16, NF)) == 1, S * PH - 1, -1)
    s = (S - 1) * rng.integers(0, 2, (N, 8, NF)); f = (NF - 1) * rng.integers(0, 2, (N, 8, NF)); c = (S - 1) * rng.integers(0, 2, (N, 8, NF))
    th = np.full((N, 8, 16, 1), 4080, np.int64)
    for a in range(N):
        for g in range(8):
            if g == 7: z = rng.permutation(15)[:9 if a % 2 == 0 else 7]
            else: z = rng.permutation(16)[:16 if g == 6 else 8]
            th[a, g, z, 0] = 0
    s[:, :, NF - 1] = S - 1; f[:, :, NF - 1] = NF - 1; c[:, :, NF - 1] = 0
    tk[::2, :, :, S - 1] = 2 * S - 1; tk[::2, :, :, 0] = 0; tk[:, 7, :, S - 1] = 2 * S - 1; tk[:, 7, :, 0] = 0
    x[..., place(S - 1, PH - 1)] = 255; x[..., place(S - 1, NF - 1)] = 255; x[..., place(0, NF - 1)] = 0
    return pack(x, tk, fr, th, s, f, c)
def setup_inputs_corners(rng):
    x, th = records(rng); tk, fr, s, f, c = parts(rng); i = np.arange(NF); even = i % 2 == 0
    near = np.array([[3, 21], [21, 3], [5, 19], [19, 5], [7, 9], [9, 7]])
    for a in range(N):
        o = rng.permutation(8)
        tk[a, o[0]] = tk[a, o[0]] & (S - 1); fr[a, o[0]] = -1
        tk[a, o[1]] = (tk[a, o[1]] & (S - 1)) + S; fr[a, o[1]] = -1
        tk[a, o[2]] = (tk[a, o[2]] & (S - 1)) + S
        fr[a, o[2]] = PH * rng.integers(0, S, (16, NF)) + np.where(rng.random((16, NF)) < 0.5, i, NF + i)
        f[a, o[3]] = i; fr[a, o[3]] = np.where(i % 2 == 0, -1, rng.integers(0, S * PH, (16, NF)))
        f[a, o[4]] = rng.choice(np.array([0, NF - 1]), NF); s[a, o[4]] = rng.choice(np.array([0, S - 1]), NF); c[a, o[4]] = np.where(rng.random(NF) < 0.5, s[a, o[4]], S - 1 - s[a, o[4]])
        fr[a, o[4]] = np.where(rng.random((16, NF)) < 0.4, -1, PH * rng.choice(np.array([0, S - 1]), (16, NF)) + rng.choice(np.array([0, NF - 1, NF, PH - 1]), (16, NF)))
        th[a, o[5]] = 4080; th[a, o[6]] = 0; th[a, o[7]] = 4080; th[a, o[7], rng.permutation(16)[:8]] = 0
        f[a, o[5]] = np.where(even, i, f[a, o[5]]); c[a, o[5]] = np.where(even, s[a, o[5]], c[a, o[5]]); fr[a, o[5]] = np.where(even, -1, fr[a, o[5]])
        pq = near[rng.integers(0, 6, NF)]
        s[a, o[6]] = np.where(even, S - pq[:, 0], s[a, o[6]]); c[a, o[6]] = np.where(even, S - pq[:, 1], c[a, o[6]])
    return pack(x, tk, fr, th, s, f, c)
def setup_inputs_ties(rng):
    v, th = records(rng); tk, fr, s, f, c = parts(rng)
    x = np.broadcast_to(60 * rng.integers(0, 5, (N, 8, 1, R)), (N, 8, 16, R)).copy()
    th = rng.choice(np.array([959, 960, 961, 1919, 1920, 1921]), (N, 8, 16, 1))
    off = rng.integers(0, 4, (N, 2, 16, R)) * (rng.random((N, 2, 1, R)) < 0.5)
    x[:, 1::4] = np.abs(255 * rng.integers(0, 2, (N, 2, 1, R)) - off)
    lev = np.array([0, 0, 0, 24, 24, 24, 4048, 4056, 4060, 4064, 4078, 4079, 4079, 4079, 4080, 4080])
    th[:, 1::4] = lev[np.argsort(rng.random((N, 2, 16, 1)), axis=2)]
    few = rng.integers(0, S, (N, 4, 3)); which = rng.integers(0, 3, (2, N, 4, NF))
    s[:, ::2] = np.take_along_axis(few, which[0], 2); c[:, ::2] = np.take_along_axis(few, which[1], 2); f[:, ::2] = rng.integers(0, 4, (N, 4, NF))
    return pack(x, tk, fr, th, s, f, c)
def check_inputs(d):
    bad = []
    for k, lo, hi in (("x", 0, 255), ("sk", 0, 2 * S - 1), ("fr", -1, S * PH - 1), ("th", 0, 4080), ("gs", 0, S - 1), ("gf", 0, NF - 1), ("gcl", 0, S - 1)):
        if k not in d: bad.append("no " + k); continue
        v = np.asarray(d[k]).astype(np.float64)
        if not (np.min(v) >= lo and np.max(v) <= hi): bad.append("range of " + k)
        elif np.any(v != np.floor(v)): bad.append("whole numbers in " + k)
    return bad
def reference(x, sk, fr, th, gs, gf, gcl):
    X = x.astype(np.float32).astype(np.int32).reshape(N, 8, 16, R); T = sk.astype(np.int64).reshape(N, 8, 16, S); lim = th.astype(np.int64).reshape(N, 8, 16, 1)
    own = fr.astype(np.int64).reshape(N, 8, 16, NF); F = np.concatenate([own, own], axis=3)
    i = np.arange(NF); mark = np.zeros((N, 8, 16, NF), bool); A = np.zeros((N, NF), np.int64)
    s = gs.astype(np.int64); f = gf.astype(np.int64); c = gcl.astype(np.int64); h = np.zeros_like(s) + i
    s0 = s; f0 = f; c0 = c
    def molecules(a, b):
        v = np.take_along_axis(T, a[:, :, None, :], 3); w = np.take_along_axis(F, b[:, :, None, :], 3)
        return np.where((v >= S) & (w >= 0), w, (v & (S - 1)) * PH + b[:, :, None, :]), (v >= S) & (w < 0)
    def pick(m):
        return np.take_along_axis(X, place(m >> LB, m & (PH - 1)).reshape(N, 8, 1, 16 * NF), 3)
    for rnd in range(RO):
        goal, _ = molecules(s, f); clause, hole = molecules(c, h)
        free = hole & (h == i)[:, :, None, :]; clause = np.where(free, goal, clause)
        D = np.add.reduce(np.abs(pick(goal) - pick(clause)), axis=2).astype(np.int64).reshape(N, 8, 16, NF)
        over = D > lim; clash = np.add.reduce(over.astype(np.int64), axis=2) >= 8 + (A & 1)[:, None, :]
        m = np.argmax(np.where(over, -1, D), axis=2)[:, :, None, :]
        gm = np.take_along_axis(goal, m, 2)[:, :, 0]; cm = np.take_along_axis(clause, m, 2)[:, :, 0]
        dm = np.take_along_axis(D, m, 2)[:, :, 0]; tm = np.take_along_axis(np.broadcast_to(lim, D.shape), m, 2)[:, :, 0]
        save = ~clash & (2 * dm < tm)
        bind = free & ~clash[:, :, None, :]
        own = np.where(mark & clash[:, :, None, :], -1, np.where(bind, goal, own))
        mark = (mark | bind) & ~(clash | save)[:, :, None, :]
        nxt = ((c0 * s0 >> 5) + c0 + 1) & (S - 1)
        s = np.where(clash, s0, gm >> LB); f = np.where(clash, f0, gm & (PH - 1))
        c = np.where(clash, nxt, cm >> LB); h = np.where(clash, i, cm & (PH - 1))
        s0 = np.where(save, s, s0); f0 = np.where(save, f, f0); c0 = np.where(clash, nxt, np.where(save, c, c0))
        A = np.add.reduce(clash.astype(np.int64), axis=1)
        F = np.concatenate([own, F[..., NF:]], axis=3)
        if rnd < RO - 1:
            d = 1 + rnd % (N - 1); col = np.take_along_axis(F, f[:, :, None, :], 3)
            F = np.concatenate([own, np.roll(col, d, axis=0)], axis=3); s = np.roll(s, d, axis=0); f = np.zeros_like(s) + NF + i
    return {"yf": np.where(own < 0, -1, 2 * own + mark).reshape(N, 128, NF).astype(np.float32), "yg": (PH * s + f).astype(np.float32), "yc": (PH * c + h).astype(np.float32),
            "ysg": (PH * s0 + f0).astype(np.float32), "yk": c0.astype(np.float32)}

@@ -1,0 +1,554 @@
+from concourse.mybir import AluOpType, ActivationFunctionType
+A = AluOpType
+F = ActivationFunctionType
+C0 = 592 * 2048 + 16
+CH = ((0, 256), (256, 384), (384, 512))
+MV = ((0, 256), (256, 512))
+def _sb(names, shape, d):
+    return {n: ("sbuf", shape, d) for n in names.split()}
+SCRATCH = {"xr": ("sbuf", [128, 8192], "bfloat16"), "T1": ("sbuf", [128, 1024], "float32"), "FB": ("sbuf", [128, 2560], "float32"),
+           "PR": ("sbuf", [128, 1024], "int32"), "OI": ("sbuf", [128, 1024], "int32"), "Z": ("sbuf", [128, 2048], "float16"),
+           "Ib": ("sbuf", [128, 1408], "bfloat16"), "BO": ("sbuf", [128, 384], "bfloat16"), "BY": ("sbuf", [128, 2048], "bfloat16"),
+           "row": ("sbuf", [128, 1664], "bfloat16"), "it": ("sbuf", [128, 640], "int32"), "il": ("sbuf", [128, 128], "int32"),
+           "If": ("sbuf", [128, 128], "float32"), "E8": ("sbuf", [128, 128], "bfloat16"), "seg": ("sbuf", [128, 256], "float32"),
+           "thi": ("sbuf", [128, 1], "int32"), "th2": ("sbuf", [128, 8], "float32"), "M16": ("sbuf", [128, 16], "float32"),
+           "Ex": ("sbuf", [128, 16], "uint16"), "lst": ("sbuf", [128, 1536], "int32"), "lsh": ("sbuf", [128, 1536], "float16"),
+           "skb": ("sbuf", [128, 1024], "int32"), "skh": ("sbuf", [128, 1024], "float16"), "skv": ("sbuf", [128, 1024], "bfloat16"),
+           "OUT": ("sbuf", [128, 2048], "float32"), "VmN": ("sbuf", [128, 144], "bfloat16"), "HC0": ("sbuf", [128, 32], "float16"), "HF": ("sbuf", [128, 64], "float16"),
+           "HF0": ("sbuf", [128, 64], "float16"), "HC": ("sbuf", [128, 64], "float16"),
+           "Vm": ("sbuf", [128, 144], "bfloat16"), "V8": ("sbuf", [128, 144], "bfloat16")}
+SCRATCH.update(_sb("U Df", [128, 8192], "bfloat16"))
+SCRATCH.update(_sb("AG AC bR cand keep Dc Mx kS col CI CB yv yr ab", [128, 512], "float32"))
+SCRATCH.update(_sb("XG XC EG PG QG PC QC frb ai oi lo", [128, 512], "int32"))
+SCRATCH.update(_sb("OG OC", [128, 512], "uint16"))
+SCRATCH.update(_sb("nfr mu sgn sg2 sc a2 oh zb", [128, 512], "bfloat16"))
+SCRATCH.update(_sb("SF0 NXH cl2 dd SF cz CM CHd zz tq nx", [128, 64], "float32"))
+SCRATCH.update(_sb("IL CP0 m1", [128, 32], "float32"))
+SCRATCH.update(_sb("nxi fxi", [128, 32], "int32"))
+SCRATCH.update(_sb("eqb", [128, 32], "bfloat16"))
+SCRATCH.update(_sb("hb", [128, 32], "float16"))
+SCRATCH.update(_sb("FL SL CL HL S1 S2", [128, 32], "uint16"))
+for _b in range(8):
+    SCRATCH["p%d" % _b] = ("psum", [128, 512], "float32")
+SEMAPHORES = ["sV", "sS", "sT", "sG"] + ["ld%d" % j for j in range(9)] + ["st%d" % j for j in range(8)]
+for _t in range(2):
+    SEMAPHORES += ["as%d" % _t, "ls%d" % _t] + ["%s%d%d" % (n, _t, b) for n in ("ac", "lc") for b in range(len(MV))]
+
+
+def rank_program(g, core, T, topo):
+    rank = T.rank_of(core)
+    if rank is None:
+        return
+    ENG = {"V": g.vector, "S": g.scalar, "T": g.tensor, "G": g, "Y": g.sync}
+    known = {e: {} for e in ENG}
+    cnt, hist = {}, {}
+
+    def bank(n):
+        return n[0] == "p" and n[1:].isdigit()
+
+    def touch(e, rd, wr):
+        toks = []
+        for regs, w in ((rd, 0), (wr, 1)):
+            for (n, a, b) in regs:
+                for (ha, hb, tok, hw, he) in hist.get(n, []):
+                    if he == e and e == "T":
+                        continue
+                    if bank(n):
+                        if he != e or hw or w:
+                            toks.append(tok)
+                    elif ha < b and a < hb and (w or hw):
+                        toks.append(tok)
+        best = {}
+        for tok in toks:
+            if known[e].get(tok[0], 0) < tok[1] and (tok[0] not in best or best[tok[0]][1] < tok[1]):
+                best[tok[0]] = tok
+        todo = [t for t in best.values() if not any(o is not t and o[2].get(t[0], 0) >= t[1] for o in best.values())]
+        for t in todo:
+            ENG[e].wait_ge(T.sem[t[0]], t[1])
+            for s, v in list(t[2].items()) + [(t[0], t[1])]:
+                known[e][s] = max(known[e].get(s, 0), v)
+
+    def note(e, tok, rd, wr):
+        for regs, w in ((rd, 0), (wr, 1)):
+            for (n, a, b) in regs:
+                h = hist.setdefault(n, [])
+                if bank(n):
+                    h[:] = [(0, 512, tok, any(x[3] for x in h if x[4] == e) or w, e)]
+                    continue
+                if w:
+                    h[:] = [x for x in h if not (a <= x[0] and x[1] <= b)]
+                else:
+                    h[:] = [x for x in h if not (x[4] == e and not x[3] and a <= x[0] and x[1] <= b)]
+                h.append((a, b, tok, w, e))
+
+    def op(e, f, rd, wr, sem=None, inc=1):
+        touch(e, rd, wr)
+        s = sem or "s" + e
+        cnt[s] = cnt.get(s, 0) + inc
+        f().then_inc(T.sem[s], inc)
+        note(e if sem is None else sem, (s, cnt[s], dict(known[e])), rd, wr)
+
+    def v(n, a=0, b=None, st=1, p=128):
+        b = T[n].shape[1] if b is None else b
+        return (T[n][0:p, a:b:st] if st > 1 else T[n][0:p, a:b], [(n, a, b)])
+
+    def ind(win, off):
+        return (win[0].indirect(off[0]), win[1] + off[1])
+
+    def tt(o, x, y, f):
+        op("V", lambda: g.vector.tensor_tensor(o[0], x[0], y[0], f), x[1] + y[1], o[1])
+
+    def ts(o, x, s1, f0, s2=None, f1=None):
+        rd = x[1] + (s1[1] if isinstance(s1, tuple) else [])
+        q1 = s1[0] if isinstance(s1, tuple) else s1
+        if f1 is None:
+            op("V", lambda: g.vector.tensor_scalar(o[0], x[0], q1, None, f0), rd, o[1])
+        else:
+            op("V", lambda: g.vector.tensor_scalar(o[0], x[0], q1, s2, f0, f1), rd, o[1])
+
+    def cp(o, x):
+        op("V", lambda: g.vector.tensor_copy(o[0], x[0]), x[1], o[1])
+
+    def fill(o, c):
+        op("V", lambda: g.vector.memset(o[0], c), [], o[1])
+
+    def act(o, x, f, bias=0.0, scale=1.0):
+        rd = x[1] + [r for c in (bias, scale) if isinstance(c, tuple) for r in c[1]]
+        bb, cc = [c[0] if isinstance(c, tuple) else c for c in (bias, scale)]
+        op("S", lambda: g.scalar.activation(o[0], x[0], f, bias=bb, scale=cc), rd, o[1])
+
+    def mm(groups):
+        def f():
+            ins = None
+            for o, prs in groups:
+                for j, (l, r) in enumerate(prs):
+                    ins = g.tensor.matmul(o[0], l[0], r[0], j == 0, j == len(prs) - 1)
+            return ins
+        op("T", f, [x for o, prs in groups for l, r in prs for x in l[1] + r[1]], [x for o, prs in groups for x in o[1]])
+
+    def iota(o, pattern, base, ch):
+        op("G", lambda: g.iota(o[0], pattern, base, ch), [], o[1])
+
+    nld = [0, 0]
+
+    def load(o, src, e="Y"):
+        s = "ld%d" % nld[0]
+        nld[0] += 1
+        op(e, lambda: ENG[e].dma_start(o[0], src), [], o[1], s, 16)
+
+    def store(dst, src, e="Y"):
+        s = "st%d" % nld[1]
+        nld[1] += 1
+        op(e, lambda: ENG[e].dma_start(dst, src[0]), src[1], [], s, 16)
+
+    load(v("lst", 0, 512, 1, 8), T.gs[:], "S")
+    load(v("frb"), T.fr[:])
+    load(v("lst", 512, 1024, 1, 8), T.gf[:], "S")
+    load(v("skb"), T.sk[:])
+    load(v("lst", 1024, 1536, 1, 8), T.gcl[:], "S")
+    load(v("xr", 592, 8192), T.x[:, 0:7600])
+    load(v("xr", 0, 592), T.x[:, 7600:8192])
+    load(v("thi"), T.th[:])
+
+    iota(v("it", 0, 128), [[-1, 128]], 0, 1)
+    iota(v("it", 384, 512), [[1, 8], [0, 16]], 0, -1)
+    iota(v("it", 256, 384), [[0, 128]], 0, 1)
+    iota(v("it", 128, 256), [[1, 8], [0, 16]], 0, 0)
+    iota(v("il", 0, 16), [[-1, 16]], 16, 1)
+    iota(v("oi"), [[1, 512]], 512, 0)
+    iota(v("il", 16, 32), [[16, 16]], 15, 0)
+    iota(v("il", 32, 64), [[16, 32]], 16, 0)
+    iota(v("il", 64, 96), [[0, 32]], 0, 1)
+    iota(v("it", 512, 640), [[0, 8], [-1, 16]], 16, 0)
+    ONE = v("Ib", 0, 128)
+
+    def IM(j):
+        return v("Ib", 128 * j, 128 * j + 128)
+    BO, NBO, ONES = v("BO", 0, 128), v("BO", 128, 256), v("BO", 256, 384)
+    R1 = v("row", 256, 384, 1, 1)
+    ts(ONE, v("it", 0, 128), 0, A.is_equal)
+    fill(v("V8", 0, 144, 1, 8), 0.0)
+    cp(v("V8", 15, 143, 16, 8), v("Ib", 0, 8, 1, 8))
+    ts(v("E8", 0, 128, 1, 8), v("it", 384, 512, 1, 8), 0, A.is_equal)
+    ts(v("it", 256, 384), v("it", 256, 384), 4, A.arith_shift_right)
+    tt(BO, v("it", 128, 256), v("it", 256, 384), A.is_equal)
+    ts(v("il", 0, 16), v("il", 0, 16), 15, A.bitwise_and)
+    ts(v("M16"), v("il", 0, 16), 0, A.is_equal)
+    fill(v("Vm"), 0.0)
+    cp(v("Vm", 15, 143, 16), v("BO", 0, 128, 16))
+    fill(v("row", 256, 384), 1.0)
+    act(v("VmN"), v("Vm"), F.Copy, 0.0, -1.0)
+    for j, c in ((8, 2048.0), (9, float((1 << 24) + (1 << 21))), (1, 65536.0), (2, 4096.0), (3, float(-(1 << 24))), (4, float(-(1 << 23))),
+                 (5, -1.0), (6, float(-3 * (1 << 23))), (7, 1024.0), (10, -2.0)):
+        act(IM(j), ONE, F.Copy, 0.0, c)
+    act(v("If"), ONE, F.Copy)
+    act(NBO, BO, F.Copy, 0.0, -2.0)
+
+    def by(y):
+        act(v("BY", 128 * y, 128 * y + 128), BO, F.Identity, 0.0, v("M16", y, y + 1))
+    for y in range(8):
+        by(y)
+    cp(v("CI"), v("oi"))
+    cp(v("lsh", 0, 1024, 1, 8), v("lst", 0, 1024, 1, 8))
+    mm([(v("p5", 0, 64), [(v("V8", 15 - q, 143 - q, 1, 8), v("lsh", q, 1024, 16, 8)) for q in range(16)])])
+    mm([(v("p4"), [(v("E8", 0, 128, 1, 8), v("lsh", 512, 1024, 1, 8))])])
+    act(v("bR"), v("p4"), F.Copy)
+    act(v("row", 640, 1152), v("bR"), F.Copy, float(1 << 24), 0.0)
+    act(v("row", 1152, 1664), v("bR"), F.Copy, float(-(1 << 23)), 0.0)
+    ts(v("lo"), v("frb"), 1023, A.bitwise_and)
+    ts(v("p3"), v("frb"), 2.0, A.mult, float(C0), A.add)
+    tt(v("yv"), v("p3"), v("lo"), A.subtract)
+    for j in range(2):
+        c = (512 * j, 512 * j + 512)
+        q = "p%d" % (6 + j)
+        cp(v("skh", *c), v("skb", *c))
+        ts(v("skv", *c), v("skh", *c), 1024.0, A.is_lt)
+        mm([(v(q), [(IM(8), v("skh", *c)), (IM(9), v("skv", *c))])])
+        act(v("T1", *c), v(q), F.Copy, float(C0 - (1 << 21) - (1 << 22)))
+    ts(v("p3"), v("yv"), float(C0), A.is_lt, float(-(1 << 23) - C0 + 1025), A.mult)
+    tt(v("FB", 0, 512), v("yv"), v("p3"), A.add)
+    cp(v("SL"), v("p5", 0, 32))
+    cp(v("FL"), v("p5", 32, 64))
+    act(v("CB"), v("CI"), F.Copy, float(-512 - (1 << 23)))
+    for y in range(8, 16):
+        by(y)
+
+    def clauses():
+        cp(v("lsh", 1024, 1536, 1, 8), v("lst", 1024, 1536, 1, 8))
+        mm([(v("p5", 64, 96), [(v("V8", 15 - q, 143 - q, 1, 8), v("lsh", 1024 + q, 1536, 16, 8)) for q in range(16)])])
+
+    def constants_a():
+        cp(v("CL"), v("p5", 64, 96))
+        ts(v("SF0", 0, 32), v("p5", 0, 32), 592.0, A.add)
+        ts(v("SF0", 32, 64), v("p5", 32, 64), 16.0, A.add)
+        ts(v("CP0"), v("p5", 64, 96), 592.0, A.add)
+
+    def constants_b():
+        ts(v("th2", 0, 1), v("thi"), 4096.5, A.add)
+        ts(v("th2", 1, 2), v("thi"), -0.5, A.add)
+        fill(v("th2", 2, 3), -2.0)
+        fill(v("th2", 3, 4), -1.0)
+        fill(v("th2", 4, 5), float(-C0 - 15))
+        fill(ONES, 1.0)
+        cp(v("Ex"), v("il", 16, 32))
+        fill(v("seg"), 1.0)
+        fill(v("seg", 0, 256, 16), 0.0)
+        cp(v("row", 0, 128), v("it", 512, 640))
+        ts(v("il", 64, 96), v("il", 64, 96), 15, A.bitwise_and)
+        tt(v("IL"), v("il", 64, 96), v("il", 32, 64), A.add)
+        cp(v("NXH", 32, 64), v("IL"))
+
+
+    def Wq(q):
+        return v("Vm", 15 - q, 143 - q)
+
+    def offs(a, e, X, P, Q, O):
+        h = 0 if O == "OG" else 512
+        ts(v(P, a, e), v(X, a, e), 11, A.arith_shift_right, 2047, A.bitwise_and)
+        ts(v(Q, a, e), v(X, a, e), 2047, A.bitwise_and)
+        tt(v("PR", h + a, h + e), v(P, a, e), v(Q, a, e), A.mult)
+        ts(v("OI", h + a, h + e), v("PR", h + a, h + e), 4, A.arith_shift_right, 8191, A.bitwise_and)
+        cp(v(O, a, e), v("OI", h + a, h + e))
+
+    OWN = (0, 512, 1536)
+    SLT = ("SL", "S1", "S2")
+
+    def goal_a(t, a, e):
+        tt(v("AG", a, e), ind(v("T1"), v(SLT[t], a // 16, e // 16)), v("CI", a, e) if t else v("bR", a, e), A.add)
+
+    def goal(t, a, e):
+        goal_a(t, a, e)
+        if t == 0:
+            tt(v("XG", a, e), ind(v("FB", 0, 512), v("FL", a // 16, e // 16)), v("AG", a, e), A.max)
+        else:
+            o = OWN[t] + 512
+            tt(v("XG", a, e), v("FB", o + a, o + e), v("AG", a, e), A.max)
+        offs(a, e, "XG", "PG", "QG", "OG")
+
+    def clause_a(t, a, e):
+        tt(v("AC", a, e), ind(v("T1"), v("CL", a // 16, e // 16)), v("bR", a, e) if t else v("CB", a, e), A.add)
+
+    def clause(t, a, e):
+        if t == 0:
+            clause_a(t, a, e)
+            tt(v("XC", a, e), v("FB", a, e), v("AC", a, e), A.max)
+        else:
+            tt(v("XC", a, e), ind(v("FB", OWN[t], OWN[t] + 1024), v("HL", a // 16, e // 16)), v("AC", a, e), A.max)
+        offs(a, e, "XC", "PC", "QC", "OC")
+        ts(v("nfr", a, e), v("XC", a, e), float(-(1 << 23)), A.not_equal)
+
+    def prep_mm(a, e):
+        mm([(v("p6", a, e), [(IM(3), v("nfr", a, e))])])
+
+    def own_prep(t, a, e):
+        p = v("p6", a, e)
+        ts(v("EG", a, e), v("XG", a, e), (1 << 22) - 1, A.bitwise_and)
+        tt(p, v("EG", a, e), p, A.add)
+        tt(v("cand", a, e), v("FB", OWN[t] + a, OWN[t] + e), p, A.max)
+
+    def grec(j):
+        act(v("U", 2048 * j, 2048 * j + 2048), ind(v("xr"), v("OG", 128 * j, 128 * j + 128)), F.Copy)
+
+    def crec(j, lo=0, n=128):
+        a, e = 128 * j + lo, 128 * j + lo + n
+        tt(v("Df", 16 * a, 16 * e), ind(v("xr"), v("OC", a, e)), v("U", 16 * a, 16 * e), A.subtract)
+
+    def absd(j, lo=0, n=128):
+        a, e = 128 * j + lo, 128 * j + lo + n
+        act(v("Df", 16 * a, 16 * e), v("Df", 16 * a, 16 * e), F.Abs)
+        dsum(a, e)
+
+    def crec_s(j):
+        act(v("Df", 2048 * j, 2048 * j + 2048), ind(v("xr"), v("OC", 128 * j, 128 * j + 128)), F.Copy)
+        for m in range(4):
+            c = (2048 * j + 512 * m, 2048 * j + 512 * m + 512)
+            p = v("p7" if m % 2 else "p1")
+            mm([(p, [(ONE, v("Df", *c)), (IM(5), v("U", *c))])])
+            act(v("Df", *c), p, F.Abs)
+        dsum(128 * j, 128 * j + 128)
+
+    def crec_r(j):
+        c = (2048 * j, 2048 * j + 2048)
+        crec(j)
+        ts(v("U", *c), v("Df", *c), 0.0, A.max, 2.0, A.mult)
+        a = 128 * j
+        mm([(v(dbank(a), a, a + 128),
+             [(v("VmN", 15 - k, 143 - k), v("Df", 16 * a + k, 16 * a + 2048, 16)) for k in range(16)]
+             + [(Wq(k), v("U", 16 * a + k, 16 * a + 2048, 16)) for k in range(16)] + [(IM(2), v("nfr", a, a + 128))])])
+
+    def dbank(a):
+        return "p0" if a < CH[0][1] else "p1" if a < CH[1][1] else "p7"
+
+    def dsum(a, e):
+        mm([(v(dbank(a), a, e), [(Wq(k), v("Df", 16 * a + k, 16 * e, 16)) for k in range(16)] + [(IM(2), v("nfr", a, e))])])
+
+    def keys(t, a, e):
+        D = v(dbank(a), a, e)
+        act(v("sgn", a, e), D, F.Sign, v("th2", 0, 1), -1.0)
+        act(v("Dc", a, e), D, F.Relu, -65536.0, 16.0)
+        mm([(v("p4", a, e), [(BO, v("sgn", a, e))] + ([(IM(10), v("a2", a, e))] if t else []))])
+        mm([(v("p2", m, m + 128), [(v("Dc", m, m + 128), v("If")), (R1, v("row", 0, 128, 1, 1)),
+                                   (v("sgn", m, m + 128), IM(1))]) for m in range(a, e, 128)])
+
+    def keys_b(t, a, e):
+        act(v("kS", a, e), v("p2", a, e), F.Copy)
+        act(v("sc", a, e), v("p4", a, e), F.Sign, -1.0 if t else 1.0, -1.0)
+        mm([(v("p4", a, e), [(IM(4), v("sc", a, e)), (R1, v("row", 1152 + a, 1152 + e, 1, 1))])])
+
+    def best(t, a, e):
+        op("V", lambda: g.vector.tensor_tensor_scan(v("Mx", a, e)[0], v("seg", 0, e - a)[0], v("kS", a, e)[0], 0.0, A.mult, A.max),
+           [("seg", 0, 256), ("kS", a, e)], [("Mx", a, e)])
+        tt(v("oh", a, e), ind(v("Mx", a, e), v("Ex", 0, (e - a) // 16)), v("kS", a, e), A.is_equal)
+        mm([(v("p3", m, m + 128), [(v("oh", m, m + 128), ONE)]) for m in range(a, e, 128)])
+
+    def saves():
+        act(v("sg2"), v("Dc"), F.Sign, v("th2", 1, 2), -0.125)
+        mm([(v("p0", m, m + 128), [(v("oh", m, m + 128), ONE), (ONE, v("sg2", m, m + 128))]) for m in range(0, 512, 128)])
+        act(v("zb"), v("p0"), F.Relu, -1.0)
+
+    def zcol(a, e, j, n):
+        tt(v("Z", 512 * j + a, 512 * j + e), v(n, a, e), v("p3", a, e), A.mult)
+
+    def lsum(p, o, n, a, e):
+        return (v(p, o, o + (e - a) // 16), [(Wq(q), v(n, a + q, e, 16)) for q in range(16)])
+
+    def choose_goal(t, a, e):
+        zcol(a, e, 1, "QG")
+        zcol(a, e, 0, "PG")
+
+    def choose_clause(t, a, e):
+        zcol(a, e, 2, "PC")
+        zcol(a, e, 3, "QC")
+
+    def own_new(t, a, e):
+        p = v("p4", a, e)
+        tt(p, v("cand", a, e), p, A.add)
+        o = v("FB", OWN[t + 1] + a, OWN[t + 1] + e) if t < 2 else v("oi", a, e)
+        tt(o, v("keep", a, e) if t else v("FB", a, e), p, A.max)
+
+    def marks(t, a, e):
+        prs = [(IM(5), v("nfr", a, e)), (NBO, v("zb", a, e)), (IM(5), v("sc", a, e))]
+        if t:
+            prs.append((ONE, v("mu", a, e)))
+        mm([(v("p4", a, e), prs)])
+        act(v("p4" if t == 2 else "mu", a, e), v("p4", a, e), F.Relu)
+        if t == 2:
+            act(v("p4", a, e), v("p4", a, e), F.Copy, -1.0)
+
+    LAST = ("S", "S", "H")
+
+    def lists_goal(t):
+        c2, d, G2 = v("cl2"), v("dd"), v("p5", 0, 64)
+        ts(v("cl2", 0, 32), v("p5", 128, 160), 0.0, A.is_gt)
+        ts(v("cl2", 32, 64), v("p5", 128, 160), 0.0, A.is_gt)
+        tt(d, v("SF0"), G2, A.subtract)
+        tt(d, d, c2, A.mult)
+        tt(v(LAST[t] + "F"), d, G2, A.add)
+        if t < 2:
+            ts(v("SL"), v("SF", 0, 32), -592.0, A.add)
+            ts(v("fxi"), v("SF", 32, 64), 496.0, A.add)
+            ts(v("fxi"), v("fxi"), 1023, A.bitwise_and)
+            cp(v("FL"), v("fxi"))
+
+    def lists_clause(t):
+        d, ch, c2, m = v("cz"), v("CHd" if t < 2 else "HC"), v("cl2"), v("m1")
+        ts(d, v("p6", 0, 64), 0.0, A.is_equal)
+        tt(d, d, v("p5", 0, 64), A.mult)
+        tt(v("CM"), d, v("p6", 0, 64), A.add)
+        tt(d, v("NXH"), v("CM"), A.subtract)
+        tt(d, d, c2, A.mult)
+        tt(ch, d, v("CM"), A.add)
+        if t < 2:
+            ts(v("CL"), v("CHd", 0, 32), -592.0, A.add)
+            ts(v("hb"), v("CHd", 32, 64), -16.0, A.add)
+            tt(m, v("CHd", 32, 64), v("IL"), A.is_equal)
+            ts(v("eqb"), m, float(-(1 << 23)), A.mult)
+            ts(v("HL"), v("CHd", 32, 64), -16.0, A.add)
+
+    def lists_save(t):
+        q, c2 = v("tq"), v("cl2")
+        tt(v("zz"), v("p6", 64, 128), c2, A.is_gt)
+        tt(q, v(LAST[t] + "F"), v("SF0"), A.subtract)
+        tt(q, q, v("zz"), A.mult)
+        tt(v(LAST[t] + "F0"), v("SF0"), q, A.add)
+
+    def save_c0(t):
+        m = v("m1")
+        tt(m, v("zz", 0, 32), v("cl2", 0, 32), A.add)
+        tt(v("tq", 0, 32), v("CHd" if t < 2 else "HC", 0, 32), v("CP0"), A.subtract)
+        tt(m, m, v("tq", 0, 32), A.mult)
+        tt(v("CP0" if t < 2 else "HC0"), v("CP0"), m, A.add)
+
+    def next_clash():
+        n, s, i = v("nx", 0, 32), v("nx", 32, 64), v("nxi")
+        ts(n, v("CP0"), -592.0, A.add)
+        ts(s, v("SF0", 0, 32), -592.0, A.add)
+        tt(i, n, s, A.mult)
+        ts(i, i, 5, A.arith_shift_right)
+        ts(n, n, 1.0, A.add)
+        tt(i, i, n, A.add)
+        ts(i, i, 1023, A.bitwise_and)
+        ts(v("NXH", 0, 32), i, 592.0, A.add)
+
+    def send(t, dst_view, src_view, rs, ls):
+        dst = T.cores[(rank + t + 1) % len(T.cores)]
+        rid, pid, _ = topo.addr(dst)
+        k = len(topo.engines(core, dst))
+        touch("G", src_view[1], [])
+        g.remote_dma(dst_view[0], src_view[0], T.sem[rs], T.sem[ls], pid, rid, topo.mask(core, dst))
+        cnt[ls] = k
+        note(ls, (ls, k, dict(known["G"])), src_view[1], [])
+        src = T.cores[(rank - t - 1) % len(T.cores)]
+        cnt[rs] = len(topo.engines(src, core))
+        note(rs, (rs, cnt[rs], {}), [], dst_view[1])
+
+    def number_out(j, p, hi, lo):
+        mm([(v(p, y, 512, 16, 8), [(v("Ib", y, 128, 16), lo)] + ([(v("Ib", 896 + y, 1024, 16), hi)] if hi else []))
+            for y in range(16)])
+        act(v("OUT", 512 * j, 512 * j + 512, 1, 8), v(p, 0, 512, 1, 8), F.Copy, float(-592 * 1024 - 16) if hi else -592.0)
+        store(T[("yg", "yc", "ysg", "yk")[j]][:], v("OUT", 512 * j, 512 * j + 512, 1, 8))
+
+    def frames_out(a, e):
+        y = v("yv", a, e)
+        ts(v("lo", a, e), v("oi", a, e), 2047, A.bitwise_and)
+        tt(y, v("oi", a, e), v("lo", a, e), A.add)
+        act(y, y, F.Relu, v("th2", 4, 5))
+
+    def frames_end(a, e):
+        tt(v("yr", a, e), v("yv", a, e), v("p4", a, e), A.add)
+        store(T.yf[:, a:e], v("yr", a, e))
+
+    H0, H1 = (0, 256), (256, 512)
+    for t in range(3):
+        for j in range(2):
+            goal(t, 128 * j, 128 * j + 128)
+            grec(j)
+            if t + j == 0:
+                clauses()
+        if t == 0:
+            constants_a()
+        if t:
+            lists_save(t - 1)
+            save_c0(t - 1)
+            for c in (H0, H1):
+                clause_a(t, *c)
+        clause(t, *H0)
+        prep_mm(*H0)
+        crec_s(0)
+        goal(t, *H1)
+        grec(2)
+        own_prep(t, *H0)
+        clause(t, *H1)
+        prep_mm(*H1)
+        crec_r(1)
+        grec(3)
+        if t == 0:
+            constants_b()
+        keys(t, *CH[0])
+        crec(2)
+        absd(2)
+        crec(3, 0, 64)
+        keys_b(t, *CH[0])
+        crec(3, 64, 64)
+        absd(3, 0, 64)
+        if t:
+            tt(v("keep"), v("FB", OWN[t], OWN[t] + 512), v("p3"), A.min)
+        best(t, *CH[0])
+        keys(t, *CH[1])
+        absd(3, 64, 64)
+        own_prep(t, *H1)
+        choose_goal(t, *CH[0])
+        own_new(t, *CH[0])
+        keys_b(t, *CH[1])
+        keys(t, *CH[2])
+        best(t, *CH[1])
+        next_clash()
+        keys_b(t, *CH[2])
+        choose_goal(t, *CH[1])
+        mm([lsum("p5", 128, "sc", 0, 512)])
+        if t == 2:
+            frames_out(*CH[0])
+        best(t, *CH[2])
+        own_new(t, *CH[1])
+        choose_goal(t, *CH[2])
+        mm([lsum("p5", 0, "Z", 0, 1024)])
+        own_new(t, *CH[2])
+        lists_goal(t)
+        saves()
+        if t < 2:
+            send(t, v(SLT[t + 1]), v("SL"), "as%d" % t, "ls%d" % t)
+            first = (0, 1024)[t]
+            o = OWN[t + 1] + 512
+            for b, (a, e) in enumerate(MV):
+                cp(v("col", a, e), ind(v("FB", first, first + 1024), v("FL", a // 16, e // 16)))
+                send(t, v("FB", o + a, o + e), v("col", a, e), "ac%d%d" % (t, b), "lc%d%d" % (t, b))
+        else:
+            number_out(0, "p1", v("HF", 0, 32), v("HF", 32, 64))
+        choose_clause(t, 0, 512)
+        mm([lsum("p6", 0, "Z", 1024, 2048)])
+        if t < 2:
+            mm([(v("p7"), [(ONES, v("sc"))])])
+            act(v("ab"), v("p7"), F.Abs, 0.0, 1.0 / 32)
+            act(v("ab"), v("ab"), F.Abs, v("th2", 2, 3))
+            act(v("a2"), v("ab"), F.Abs, v("th2", 3, 4))
+        if t < 2:
+            marks(t, 0, 512)
+        else:
+            frames_out(*H1)
+        lists_clause(t)
+        if t < 2:
+            mm([(v("p1", y, 512, 16), [(v("BY", 128 * y, 128 * y + 128), v("hb")), (v("BY", 128 * y, 128 * y + 128), v("eqb"))]) for y in range(16)])
+            act(v("bR"), v("p1"), F.Copy)
+            mm([lsum("p6", 64, "zb", 0, 512), lsum("p6", 96, "zb", 0, 512)])
+            mm([(v("p3"), [(R1, v("row", 640, 1152, 1, 1)), (IM(6), v("mu"))])])
+    mm([lsum("p6", 64, "zb", 0, 512), lsum("p6", 96, "zb", 0, 512)])
+    number_out(1, "p7", v("HC", 0, 32), v("HC", 32, 64))
+    marks(2, 0, 512)
+    lists_save(2)
+    save_c0(2)
+    number_out(2, "p1", v("HF0", 0, 32), v("HF0", 32, 64))
+    number_out(3, "p2", None, v("HC0"))
+    frames_end(*H0)
+    frames_end(*H1)
+    for s in cnt:
+        g.wait_ge(T.sem[s], cnt[s])

@@ -2,37 +2,47 @@ from concourse.mybir import AluOpType, ActivationFunctionType
 A = AluOpType
 F = ActivationFunctionType
 C0 = 592 * 2048 + 16
-CH = ((0, 256), (256, 384), (384, 512))
-MV = ((0, 256), (256, 512))
+FW = 2056
+CS = ((5, 7), (5, 7), (5, 7))
+MV = ((0, 256), (256, 384), (384, 512))
+TURNS = 3
+ORDER = {}
+GATHER, WAKE, FLY, RATE = 1.56, 80, 1800, 170
+
+
 def _sb(names, shape, d):
     return {n: ("sbuf", shape, d) for n in names.split()}
-SCRATCH = {"xr": ("sbuf", [128, 8192], "bfloat16"), "T1": ("sbuf", [128, 1024], "float32"), "FB": ("sbuf", [128, 2560], "float32"),
-           "PR": ("sbuf", [128, 1024], "int32"), "OI": ("sbuf", [128, 1024], "int32"), "Z": ("sbuf", [128, 2048], "float16"),
-           "Ib": ("sbuf", [128, 1408], "bfloat16"), "BO": ("sbuf", [128, 384], "bfloat16"), "BY": ("sbuf", [128, 2048], "bfloat16"),
-           "row": ("sbuf", [128, 1664], "bfloat16"), "it": ("sbuf", [128, 640], "int32"), "il": ("sbuf", [128, 128], "int32"),
-           "If": ("sbuf", [128, 128], "float32"), "E8": ("sbuf", [128, 128], "bfloat16"), "seg": ("sbuf", [128, 256], "float32"),
-           "thi": ("sbuf", [128, 1], "int32"), "th2": ("sbuf", [128, 8], "float32"), "M16": ("sbuf", [128, 16], "float32"),
-           "Ex": ("sbuf", [128, 16], "uint16"), "lst": ("sbuf", [128, 1536], "int32"), "lsh": ("sbuf", [128, 1536], "float16"),
+
+
+SCRATCH = {"xr": ("sbuf", [128, 8192], "bfloat16"), "T12": ("sbuf", [128, 2048], "float32"), "FB": ("sbuf", [128, 2560], "float32"),
+           "RW": ("sbuf", [128, 2048], "float32"), "CI": ("sbuf", [128, 128], "int32"), "AG": ("sbuf", [128, 128], "float32"),
+           "FLAT": ("sbuf", [128, 4 * FW], "int32"), "U": ("sbuf", [128, 8192], "bfloat16"), "W2": ("sbuf", [128, 3072], "bfloat16"),
+           "D3": ("sbuf", [128, 32, 256], "bfloat16"), "R3": ("sbuf", [128, 32, 256], "bfloat16"),
+           "Ib": ("sbuf", [128, 15 * 128], "bfloat16"), "BO": ("sbuf", [128, 256], "bfloat16"), "BY": ("sbuf", [128, 4096], "bfloat16"),
+           "Vm": ("sbuf", [128, 11 * 144], "bfloat16"), "TH": ("sbuf", [128, 256], "bfloat16"), "OF": ("sbuf", [128, 128], "float16"),
+           "TK": ("sbuf", [128, 128], "float32"), "row": ("sbuf", [128, 1024], "bfloat16"), "it": ("sbuf", [128, 512], "int32"), "il": ("sbuf", [128, 64], "int32"),
+           "If": ("sbuf", [128, 128], "float32"), "seg": ("sbuf", [128, 128], "bfloat16"), "thi": ("sbuf", [128, 8], "int32"),
+           "thf": ("sbuf", [128, 8], "float32"), "M16": ("sbuf", [128, 16], "float32"), "H2": ("sbuf", [128, 128], "int32"),
            "skb": ("sbuf", [128, 1024], "int32"), "skh": ("sbuf", [128, 1024], "float16"), "skv": ("sbuf", [128, 1024], "bfloat16"),
-           "OUT": ("sbuf", [128, 2048], "float32"), "VmN": ("sbuf", [128, 144], "bfloat16"), "HC0": ("sbuf", [128, 32], "float16"), "HF": ("sbuf", [128, 64], "float16"),
-           "HF0": ("sbuf", [128, 64], "float16"), "HC": ("sbuf", [128, 64], "float16"),
-           "Vm": ("sbuf", [128, 144], "bfloat16"), "V8": ("sbuf", [128, 144], "bfloat16")}
-SCRATCH.update(_sb("U Df", [128, 8192], "bfloat16"))
-SCRATCH.update(_sb("AG AC bR cand keep Dc Mx kS col CI CB yv yr ab", [128, 512], "float32"))
-SCRATCH.update(_sb("XG XC EG PG QG PC QC frb ai oi lo", [128, 512], "int32"))
+           "LT": ("sbuf", [128, 96], "int32"), "ST": ("sbuf", [128, 96], "int32"), "SI": ("sbuf", [128, 96], "int32"),
+           "LF": ("sbuf", [128, 96], "float32"), "LL": ("sbuf", [128, 96], "float32"), "OUT": ("sbuf", [128, 128], "float32"),
+           "nw": ("sbuf", [128, 128], "float16"), "Zc": ("sbuf", [128, 128], "float16"), "sv": ("sbuf", [128, 96], "float16"),
+           "IH": ("sbuf", [128, 96], "float16"), "res": ("sbuf", [128, 512], "float16")}
+SCRATCH.update(_sb("Ts Tc Fg A2 EF keep Mn km yv yr", [128, 512], "float32"))
+SCRATCH.update(_sb("XG XC EG PG QG PC QC PRG PRC OIG OIC frb lo oi", [128, 512], "int32"))
 SCRATCH.update(_sb("OG OC", [128, 512], "uint16"))
-SCRATCH.update(_sb("nfr mu sgn sg2 sc a2 oh zb", [128, 512], "bfloat16"))
-SCRATCH.update(_sb("SF0 NXH cl2 dd SF cz CM CHd zz tq nx", [128, 64], "float32"))
-SCRATCH.update(_sb("IL CP0 m1", [128, 32], "float32"))
-SCRATCH.update(_sb("nxi fxi", [128, 32], "int32"))
-SCRATCH.update(_sb("eqb", [128, 32], "bfloat16"))
-SCRATCH.update(_sb("hb", [128, 32], "float16"))
-SCRATCH.update(_sb("FL SL CL HL S1 S2", [128, 32], "uint16"))
-for _b in range(8):
-    SCRATCH["p%d" % _b] = ("psum", [128, 512], "float32")
-SEMAPHORES = ["sV", "sS", "sT", "sG"] + ["ld%d" % j for j in range(9)] + ["st%d" % j for j in range(8)]
+SCRATCH.update(_sb("sgf mu sg Cn", [128, 512], "bfloat16"))
+SCRATCH.update(_sb("PH QH", [128, 512], "float16"))
+SCRATCH.update(_sb("kf ko ai av NX n1 n2", [128, 32], "int32"))
+SCRATCH.update(_sb("cl ncl ncs eq", [128, 32], "bfloat16"))
+SCRATCH.update(_sb("CL HL ML", [128, 32], "uint16"))
+SCRATCH.update(_sb("L0 L1 L2 LS", [128, 64], "uint16"))
+for _b in ("A0", "A1", "C", "K0", "K1", "K2", "M", "N"):
+    SCRATCH["p" + _b] = ("psum", [128, 512], "float32")
+SEMAPHORES = ["sV", "sS", "sT", "sG"] + ["ld%d" % j for j in range(12)] + ["st%d" % j for j in range(12)]
+SEMAPHORES += ["fl%d" % j for j in range(4)] + ["h2"]
 for _t in range(2):
-    SEMAPHORES += ["as%d" % _t, "ls%d" % _t] + ["%s%d%d" % (n, _t, b) for n in ("ac", "lc") for b in range(len(MV))]
+    SEMAPHORES += ["as%d" % _t, "ls%d" % _t, "ag%d" % _t, "lg%d" % _t] + ["%s%d%d" % (n, _t, b) for n in ("ac", "lc") for b in range(len(MV))]
 
 
 def rank_program(g, core, T, topo):
@@ -44,7 +54,7 @@ def rank_program(g, core, T, topo):
     cnt, hist = {}, {}
 
     def bank(n):
-        return n[0] == "p" and n[1:].isdigit()
+        return n[0] == "p" and n[1].isupper()
 
     def touch(e, rd, wr):
         toks = []
@@ -65,8 +75,8 @@ def rank_program(g, core, T, topo):
         todo = [t for t in best.values() if not any(o is not t and o[2].get(t[0], 0) >= t[1] for o in best.values())]
         for t in todo:
             ENG[e].wait_ge(T.sem[t[0]], t[1])
-            for s, v in list(t[2].items()) + [(t[0], t[1])]:
-                known[e][s] = max(known[e].get(s, 0), v)
+            for s, c in list(t[2].items()) + [(t[0], t[1])]:
+                known[e][s] = max(known[e].get(s, 0), c)
 
     def note(e, tok, rd, wr):
         for regs, w in ((rd, 0), (wr, 1)):
@@ -81,356 +91,477 @@ def rank_program(g, core, T, topo):
                     h[:] = [x for x in h if not (x[4] == e and not x[3] and a <= x[0] and x[1] <= b)]
                 h.append((a, b, tok, w, e))
 
-    def op(e, f, rd, wr, sem=None, inc=1):
-        touch(e, rd, wr)
-        s = sem or "s" + e
-        cnt[s] = cnt.get(s, 0) + inc
-        f().then_inc(T.sem[s], inc)
-        note(e if sem is None else sem, (s, cnt[s], dict(known[e])), rd, wr)
+    calls = []
+
+    def op(e, f, rd, wr, cyc, sem=None, upto=None, moved=0):
+        def issue():
+            touch(e, rd, wr)
+            s, inc = sem or "s" + e, 16 if sem else 1
+            cnt[s] = cnt.get(s, 0) + inc
+            f().then_inc(T.sem[s], inc)
+            note(e if sem is None else sem, (s, upto or cnt[s], dict(known[e])), rd, wr)
+        calls.append((e, issue, rd, wr, cyc, moved))
+
+    def issue_all():
+        n = len(calls)
+        pre, seen = [set() for _ in calls], {}
+        for i, (e, f, rd, wr, cyc, moved) in enumerate(calls):
+            for regs, w in ((rd, 0), (wr, 1)):
+                for (x, a, b) in regs:
+                    h = seen.setdefault(x, [])
+                    if bank(x):
+                        a, b, w = 0, 512, 1
+                    pre[i].update(j for (ha, hb, j, hw) in h if ha < b and a < hb and (w or hw) and j != i)
+                    if w:
+                        h[:] = [y for y in h if not (a <= y[0] and y[1] <= b)]
+                    h.append((a, b, i, w))
+        post = [[] for _ in calls]
+        for i in range(n):
+            for j in pre[i]:
+                post[j].append(i)
+        q, cyc = [c[0] for c in calls], [c[4] for c in calls]
+        fly = [FLY + c[5] / RATE if c[5] else 0 for c in calls]
+
+        def plan(pre, post, rest, back):
+            left, free, order, ends = [len(p) for p in pre], {e: 0.0 for e in "VSTGYD"}, [], [0.0] * n
+            ready = [fly[i] if back else 0.0 for i in range(n)]
+            todo = [i for i in range(n) if not left[i]]
+            while todo:
+                first = min(todo, key=lambda i: max(ready[i], free[q[i]]) + cyc[i])
+                e = q[first]
+                end = max(ready[first], free[e]) + cyc[first]
+                i = max((j for j in todo if q[j] == e and max(ready[j], free[e]) < end), key=lambda j: rest[j] - max(ready[j] - free[e], 0))
+                todo.remove(i)
+                order.append(i)
+                free[e] = ends[i] = done = max(ready[i], free[e]) + cyc[i]
+                if fly[i] and not back:
+                    free["D"] = max(free["D"], done + FLY / 2) + fly[i] - FLY
+                    done = free["D"] + FLY / 2
+                for j in post[i]:
+                    ready[j] = max(ready[j], done + (fly[j] if back else 0) + (0 if q[j] == e == "T" else WAKE))
+                    left[j] -= 1
+                    if not left[j]:
+                        todo.append(j)
+            return max(ends[i] + (0 if back else fly[i]) for i in range(n)), order, ends
+        ends, best = [200.0 * i for i in range(n)], ORDER.get(n)
+        for turn in range(0 if best else TURNS):
+            rest = plan(post, pre, ends, True)[2]
+            now = plan(pre, post, [1e9 - 1e4 * i for i in range(nld[0])] + rest[nld[0]:], False)
+            ends = now[2]
+            best = min(best or now, now)
+        ORDER[n] = best
+        for i in best[1]:
+            calls[i][1]()
 
     def v(n, a=0, b=None, st=1, p=128):
         b = T[n].shape[1] if b is None else b
-        return (T[n][0:p, a:b:st] if st > 1 else T[n][0:p, a:b], [(n, a, b)])
+        return (T[n][0:p, a:b:st] if st > 1 else T[n][0:p, a:b], [(n, a, b)], (b - a + st - 1) // st)
+
+    def v3(n, a, e, r=None):
+        c, d = a // 16, e // 16
+        return (T[n][:, c:d, :] if r is None else T[n][:, c:d, 16 * r:16 * r + 16], [(n, a, e)], (e - a) * (16 if r is None else 1))
 
     def ind(win, off):
-        return (win[0].indirect(off[0]), win[1] + off[1])
+        return (win[0].indirect(off[0]), win[1] + off[1], None)
+
+    def cost(o, x, rate=None):
+        if x[2] is None:
+            return 70 + GATHER * o[2]
+        if rate is None:
+            rate = 0.5 if all(SCRATCH[y[1][0][0]][2].endswith("16") for y in (o, x)) else 1
+        return max(64, rate * o[2])
 
     def tt(o, x, y, f):
-        op("V", lambda: g.vector.tensor_tensor(o[0], x[0], y[0], f), x[1] + y[1], o[1])
+        op("V", lambda: g.vector.tensor_tensor(o[0], x[0], y[0], f), x[1] + y[1], o[1], cost(o, x, 1 if bank(x[1][0][0]) or bank(y[1][0][0]) else 2))
 
     def ts(o, x, s1, f0, s2=None, f1=None):
-        rd = x[1] + (s1[1] if isinstance(s1, tuple) else [])
-        q1 = s1[0] if isinstance(s1, tuple) else s1
+        rd = x[1] + [r for c in (s1, s2) if isinstance(c, tuple) for r in c[1]]
+        q1, q2 = [c[0] if isinstance(c, tuple) else c for c in (s1, s2)]
         if f1 is None:
-            op("V", lambda: g.vector.tensor_scalar(o[0], x[0], q1, None, f0), rd, o[1])
+            op("V", lambda: g.vector.tensor_scalar(o[0], x[0], q1, None, f0), rd, o[1], cost(o, x))
         else:
-            op("V", lambda: g.vector.tensor_scalar(o[0], x[0], q1, s2, f0, f1), rd, o[1])
+            op("V", lambda: g.vector.tensor_scalar(o[0], x[0], q1, q2, f0, f1), rd, o[1], cost(o, x))
 
-    def cp(o, x):
-        op("V", lambda: g.vector.tensor_copy(o[0], x[0]), x[1], o[1])
+    def cp(o, x, f=None):
+        op("V", lambda: g.vector.tensor_copy(o[0], x[0]), x[1], o[1], cost(o, x))
+
+    def turn(o, x):
+        op("V", lambda: g.vector.transpose(o[0], x[0]), x[1], o[1], cost(o, x))
+
+    def scan(o, x, f):
+        s = v("seg", 0, o[2])
+        op("V", lambda: g.vector.tensor_tensor_scan(o[0], s[0], x[0], 0.0, A.mult, f), s[1] + x[1], o[1], cost(o, x))
 
     def fill(o, c):
-        op("V", lambda: g.vector.memset(o[0], c), [], o[1])
+        op("V", lambda: g.vector.memset(o[0], c), [], o[1], cost(o, o))
 
     def act(o, x, f, bias=0.0, scale=1.0):
         rd = x[1] + [r for c in (bias, scale) if isinstance(c, tuple) for r in c[1]]
         bb, cc = [c[0] if isinstance(c, tuple) else c for c in (bias, scale)]
-        op("S", lambda: g.scalar.activation(o[0], x[0], f, bias=bb, scale=cc), rd, o[1])
+        op("S", lambda: g.scalar.activation(o[0], x[0], f, bias=bb, scale=cc), rd, o[1], cost(o, x, 1))
 
-    def mm(groups):
+    def mm(prods, start=True, stop=True):
         def f():
             ins = None
-            for o, prs in groups:
-                for j, (l, r) in enumerate(prs):
-                    ins = g.tensor.matmul(o[0], l[0], r[0], j == 0, j == len(prs) - 1)
+            for j, (o, l, r) in enumerate(prods):
+                ins = g.tensor.matmul(o[0], l[0], r[0], start and j == 0, stop and j == len(prods) - 1)
             return ins
-        op("T", f, [x for o, prs in groups for l, r in prs for x in l[1] + r[1]], [x for o, prs in groups for x in o[1]])
+        op("T", f, [x for o, l, r in prods for x in l[1] + r[1]], [x for o, l, r in prods for x in o[1]],
+           sum(max(64, r[2]) * (2 if l[1][0][0] == "If" else 0.5) for o, l, r in prods))
 
     def iota(o, pattern, base, ch):
-        op("G", lambda: g.iota(o[0], pattern, base, ch), [], o[1])
+        op("G", lambda: g.iota(o[0], pattern, base, ch), [], o[1], 160 + 2 * o[2])
+
+    def conv(o, x):
+        op("G", lambda: g.affine_select(o[0], x[0], [[0, o[2]]], A.is_equal, 0.0, 0, 0), x[1], o[1], 200 + 2 * o[2])
 
     nld = [0, 0]
+
+    def size(x):
+        return 128 * x[2] * (2 if SCRATCH[x[1][0][0]][2].endswith("16") else 4)
 
     def load(o, src, e="Y"):
         s = "ld%d" % nld[0]
         nld[0] += 1
-        op(e, lambda: ENG[e].dma_start(o[0], src), [], o[1], s, 16)
+        op(e, lambda: ENG[e].dma_start(o[0], src), [], o[1], 100, s, None, size(o))
 
     def store(dst, src, e="Y"):
         s = "st%d" % nld[1]
         nld[1] += 1
-        op(e, lambda: ENG[e].dma_start(dst, src[0]), src[1], [], s, 16)
+        op(e, lambda: ENG[e].dma_start(dst, src[0]), src[1], [], 100, s, None, size(src))
 
-    load(v("lst", 0, 512, 1, 8), T.gs[:], "S")
-    load(v("frb"), T.fr[:])
-    load(v("lst", 512, 1024, 1, 8), T.gf[:], "S")
+    def move(dst, src, s, upto=None):
+        op("Y", lambda: g.sync.dma_start(dst[0], src[0]), src[1], dst[1], 100, s, upto, size(src))
+
+    def flat(j, plane):
+        return (T.FLAT[plane:128:16, FW * j + 8:FW * j + FW], [("FLAT%d" % plane, j, j + 1)])
+
     load(v("skb"), T.sk[:])
-    load(v("lst", 1024, 1536, 1, 8), T.gcl[:], "S")
+    for n, src in enumerate((T.gs, T.gf, T.gcl)):
+        for h in range(2):
+            load(v("LT", 32 * n + 16 * h, 32 * n + 16 * h + 16), src[h:8:2, :], "YS"[h])
+    load(v("frb"), T.fr[:])
+    load(v("thi", 0, 1), T.th[:], "S")
     load(v("xr", 592, 8192), T.x[:, 0:7600])
     load(v("xr", 0, 592), T.x[:, 7600:8192])
-    load(v("thi"), T.th[:])
 
     iota(v("it", 0, 128), [[-1, 128]], 0, 1)
-    iota(v("it", 384, 512), [[1, 8], [0, 16]], 0, -1)
-    iota(v("it", 256, 384), [[0, 128]], 0, 1)
-    iota(v("it", 128, 256), [[1, 8], [0, 16]], 0, 0)
-    iota(v("il", 0, 16), [[-1, 16]], 16, 1)
-    iota(v("oi"), [[1, 512]], 512, 0)
-    iota(v("il", 16, 32), [[16, 16]], 15, 0)
-    iota(v("il", 32, 64), [[16, 32]], 16, 0)
-    iota(v("il", 64, 96), [[0, 32]], 0, 1)
-    iota(v("it", 512, 640), [[0, 8], [-1, 16]], 16, 0)
-    ONE = v("Ib", 0, 128)
+    iota(v("it", 128, 256), [[-16, 8], [0, 16]], 0, 1)
+    iota(v("il", 0, 32), [[16, 32]], 0, 0)
+    iota(v("il", 32, 33), [[0, 1]], 0, 1)
+    iota(v("it", 256, 384), [[16, 8], [128, 16]], -1016, 0)
+    iota(v("CI"), [[1, 128]], 512, 0)
 
-    def IM(j):
+    def window(j):
+        return (T.FLAT[:, FW * j:FW * j + FW], [("FLAT%d" % q, j, j + 1) for q in range(6)], FW)
+    for j in range(4):
+        iota(window(j), [[0, FW]], 0, 0)
+    SCALES = (1.0, None, -1.0, 2048.0, float(5 << 21), float(13 << 21), -592.0, -16.0, float(-(1 << 24)), float(1 << 23),
+              float(-(1 << 23)), float(1 << 24), -8192.0, 1024.0, -592.0 * 1024)
+
+    def IM(c):
+        j = SCALES.index(c)
         return v("Ib", 128 * j, 128 * j + 128)
-    BO, NBO, ONES = v("BO", 0, 128), v("BO", 128, 256), v("BO", 256, 384)
-    R1 = v("row", 256, 384, 1, 1)
-    ts(ONE, v("it", 0, 128), 0, A.is_equal)
-    fill(v("V8", 0, 144, 1, 8), 0.0)
-    cp(v("V8", 15, 143, 16, 8), v("Ib", 0, 8, 1, 8))
-    ts(v("E8", 0, 128, 1, 8), v("it", 384, 512, 1, 8), 0, A.is_equal)
-    ts(v("it", 256, 384), v("it", 256, 384), 4, A.arith_shift_right)
-    tt(BO, v("it", 128, 256), v("it", 256, 384), A.is_equal)
-    ts(v("il", 0, 16), v("il", 0, 16), 15, A.bitwise_and)
-    ts(v("M16"), v("il", 0, 16), 0, A.is_equal)
-    fill(v("Vm"), 0.0)
-    cp(v("Vm", 15, 143, 16), v("BO", 0, 128, 16))
-    fill(v("row", 256, 384), 1.0)
-    act(v("VmN"), v("Vm"), F.Copy, 0.0, -1.0)
-    for j, c in ((8, 2048.0), (9, float((1 << 24) + (1 << 21))), (1, 65536.0), (2, 4096.0), (3, float(-(1 << 24))), (4, float(-(1 << 23))),
-                 (5, -1.0), (6, float(-3 * (1 << 23))), (7, 1024.0), (10, -2.0)):
-        act(IM(j), ONE, F.Copy, 0.0, c)
-    act(v("If"), ONE, F.Copy)
-    act(NBO, BO, F.Copy, 0.0, -2.0)
+    ONE, W16, BO = IM(1.0), IM(None), v("BO", 0, 128)
+    ONES = v("row", 0, 512, 1, 1)
 
-    def by(y):
-        act(v("BY", 128 * y, 128 * y + 128), BO, F.Identity, 0.0, v("M16", y, y + 1))
-    for y in range(8):
-        by(y)
-    cp(v("CI"), v("oi"))
-    cp(v("lsh", 0, 1024, 1, 8), v("lst", 0, 1024, 1, 8))
-    mm([(v("p5", 0, 64), [(v("V8", 15 - q, 143 - q, 1, 8), v("lsh", q, 1024, 16, 8)) for q in range(16)])])
-    mm([(v("p4"), [(v("E8", 0, 128, 1, 8), v("lsh", 512, 1024, 1, 8))])])
-    act(v("bR"), v("p4"), F.Copy)
-    act(v("row", 640, 1152), v("bR"), F.Copy, float(1 << 24), 0.0)
-    act(v("row", 1152, 1664), v("bR"), F.Copy, float(-(1 << 23)), 0.0)
-    ts(v("lo"), v("frb"), 1023, A.bitwise_and)
-    ts(v("p3"), v("frb"), 2.0, A.mult, float(C0), A.add)
-    tt(v("yv"), v("p3"), v("lo"), A.subtract)
+    def RC(j):
+        return v("row", 512 + 128 * j, 640 + 128 * j, 1, 1)
+
+    def Wq(j, q):
+        return v("Vm", 144 * j + 15 - q, 144 * j + 143 - q)
+
+    def BY(j, y):
+        return v("BY", 2048 * j + 128 * y, 2048 * j + 128 * y + 128)
+    ts(ONE, v("it", 0, 128), 0, A.is_equal)
+    ts(v("it", 0, 128), v("it", 0, 128), 15, A.bitwise_and)
+    ts(W16, v("it", 0, 128), 0, A.is_equal)
+    ts(v("M16"), v("it", 0, 16), 0, A.is_equal)
+    ts(v("it", 128, 256), v("it", 128, 256), 4, A.arith_shift_right)
+    ts(BO, v("it", 128, 256), 0, A.is_equal)
+    for c in SCALES[3:6]:
+        act(IM(c), ONE, F.Copy, 0.0, c)
+    act(v("If"), ONE, F.Copy)
+    for y in range(16):
+        act(BY(0, y), BO, F.Identity, 0.0, v("M16", y, y + 1))
     for j in range(2):
         c = (512 * j, 512 * j + 512)
-        q = "p%d" % (6 + j)
         cp(v("skh", *c), v("skb", *c))
         ts(v("skv", *c), v("skh", *c), 1024.0, A.is_lt)
-        mm([(v(q), [(IM(8), v("skh", *c)), (IM(9), v("skv", *c))])])
-        act(v("T1", *c), v(q), F.Copy, float(C0 - (1 << 21) - (1 << 22)))
-    ts(v("p3"), v("yv"), float(C0), A.is_lt, float(-(1 << 23) - C0 + 1025), A.mult)
-    tt(v("FB", 0, 512), v("yv"), v("p3"), A.add)
-    cp(v("SL"), v("p5", 0, 32))
-    cp(v("FL"), v("p5", 32, 64))
-    act(v("CB"), v("CI"), F.Copy, float(-512 - (1 << 23)))
-    for y in range(8, 16):
-        by(y)
+        mm([(v("pA%d" % j), IM(2048.0), v("skh", *c)), (v("pA%d" % j), IM(SCALES[4]), v("skv", *c))])
+        act(v("T12", *c), v("pA%d" % j), F.Copy, float(C0 + (1 << 21)))
+    cp(v("LF"), v("LT"))
+    turn(v("LL"), v("LF"))
+    cp(v("L0"), v("LL", 0, 64))
+    cp(v("IH", 64, 96), v("LL", 32, 64))
+    ts(v("lo"), v("frb"), -(1 << 31) + (1023 << 10), A.bitwise_and)
+    ts(v("pK0"), v("frb"), float(C0 + (1 << 23)), A.add)
+    tt(v("FB", 0, 512), v("lo"), v("pK0"), A.add)
+    ts(v("CL"), v("LL", 64, 96), 1024.0, A.add)
+    ts(v("il", 32, 33), v("il", 32, 33), 15, A.bitwise_and)
+    cp(v("thf", 7, 8), v("il", 32, 33))
+    ts(v("IH", 0, 32), v("il", 0, 32), v("thf", 7, 8), A.add)
+    for j in range(2):
+        c = (512 * j, 512 * j + 512)
+        q = ("pM", "pN")[j]
+        mm([(v(q), IM(2048.0), v("skh", *c)), (v(q), IM(SCALES[5]), v("skv", *c))])
 
-    def clauses():
-        cp(v("lsh", 1024, 1536, 1, 8), v("lst", 1024, 1536, 1, 8))
-        mm([(v("p5", 64, 96), [(v("V8", 15 - q, 143 - q, 1, 8), v("lsh", 1024 + q, 1536, 16, 8)) for q in range(16)])])
+    def tables_b():
+        for j in range(2):
+            act(v("T12", 1024 + 512 * j, 1536 + 512 * j), v(("pM", "pN")[j]), F.Copy, float(C0 + (1 << 21) - (1 << 24)))
 
-    def constants_a():
-        cp(v("CL"), v("p5", 64, 96))
-        ts(v("SF0", 0, 32), v("p5", 0, 32), 592.0, A.add)
-        ts(v("SF0", 32, 64), v("p5", 32, 64), 16.0, A.add)
-        ts(v("CP0"), v("p5", 64, 96), 592.0, A.add)
-
-    def constants_b():
-        ts(v("th2", 0, 1), v("thi"), 4096.5, A.add)
-        ts(v("th2", 1, 2), v("thi"), -0.5, A.add)
-        fill(v("th2", 2, 3), -2.0)
-        fill(v("th2", 3, 4), -1.0)
-        fill(v("th2", 4, 5), float(-C0 - 15))
-        fill(ONES, 1.0)
-        cp(v("Ex"), v("il", 16, 32))
+    def constants_v():
+        fill(v("Vm", 0, 144), 0.0)
+        cp(v("Vm", 15, 143, 16), v("BO", 0, 128, 16))
+        cp(v("ST"), v("LL"))
+        ts(v("IH", 32, 64), v("IH", 0, 32), 512.0, A.add)
+        ts(v("OF"), v("it", 256, 384), v("thf", 7, 8), A.add)
         fill(v("seg"), 1.0)
-        fill(v("seg", 0, 256, 16), 0.0)
-        cp(v("row", 0, 128), v("it", 512, 640))
-        ts(v("il", 64, 96), v("il", 64, 96), 15, A.bitwise_and)
-        tt(v("IL"), v("il", 64, 96), v("il", 32, 64), A.add)
-        cp(v("NXH", 32, 64), v("IL"))
+        fill(v("seg", 0, 128, 16), 0.0)
+        fill(v("row", 0, 512, 1, 1), 1.0)
+        ts(v("thi", 1, 2), v("thi", 0, 1), 4, A.arith_shift_right)
+        ts(v("thi", 2, 3), v("thi", 0, 1), 15, A.bitwise_and)
+        ts(v("thi", 3, 4), v("thi", 0, 1), 1.0, A.add)
+        ts(v("thi", 3, 4), v("thi", 3, 4), 1, A.arith_shift_right)
+        cp(v("thf", 0, 3), v("thi", 1, 4))
+        ts(v("H2"), v("it", 0, 128), 0.0, A.mult, v("thf", 2, 3), A.add)
+        for j in range(4):
+            move(flat(j, 4), v("H2"), "h2", 64)
 
+    def constants_s():
+        for c in SCALES[2:3] + SCALES[6:]:
+            act(IM(c), ONE, F.Copy, 0.0, c)
+        for j, c in ((1, -8192.0), (2, 4096.0), (3, -4096.0)):
+            act(v("Vm", 144 * j, 144 * j + 144), v("Vm", 0, 144), F.Copy, 0.0, c)
+        for j in range(4):
+            act(v("Vm", 144 * (4 + j), 144 * (5 + j)), v("Vm", 0, 144), F.Identity, 0.0, v("M16", j, j + 1))
+        act(v("Vm", 144 * 8, 144 * 9), v("Vm", 144 * 3, 144 * 4), F.Identity, 0.0, v("M16", 4, 5))
+        for j in range(2):
+            act(v("thf", 3 + j, 4 + j), v("M16", 2 * j, 2 * j + 1), F.Identity, v("M16", 2 * j + 1, 2 * j + 2), 1024.0)
+            act(v("Vm", 144 * (9 + j), 144 * (10 + j)), v("Vm", 0, 144), F.Identity, 0.0, v("thf", 3 + j, 4 + j))
+        for j in range(2):
+            act(v("TH", 128 * j, 128 * j + 128), W16, F.Identity, 0.0, v("thf", j, j + 1))
+        act(v("BO", 128, 256), BO, F.Copy, 0.0, 16.0)
+        mm([(v("pK0", 0, 128), v("BO", 128, 256), v("TH", 0, 128)), (v("pK0", 0, 128), BO, v("TH", 128, 256))])
+        act(v("TK"), v("pK0", 0, 128), F.Copy, -4096.0, -4096.0)
+        for j, c in enumerate((float(-(1 << 24)), float(1 << 24), 4096.0, -3072.0)):
+            act(RC(j), v("row", 0, 128, 1, 1), F.Copy, 0.0, c)
+        for j in range(4):
+            act(v("BY", 2048 + 512 * j, 2560 + 512 * j), v("BY", 512 * j, 512 * j + 512), F.Copy, 0.0, float(1 << 24))
 
-    def Wq(q):
-        return v("Vm", 15 - q, 143 - q)
-
-    def offs(a, e, X, P, Q, O):
-        h = 0 if O == "OG" else 512
-        ts(v(P, a, e), v(X, a, e), 11, A.arith_shift_right, 2047, A.bitwise_and)
-        ts(v(Q, a, e), v(X, a, e), 2047, A.bitwise_and)
-        tt(v("PR", h + a, h + e), v(P, a, e), v(Q, a, e), A.mult)
-        ts(v("OI", h + a, h + e), v("PR", h + a, h + e), 4, A.arith_shift_right, 8191, A.bitwise_and)
-        cp(v(O, a, e), v("OI", h + a, h + e))
+    def spread(p, j, x, a=0, e=512):
+        return [(v(p, a + y, e, 16), BY(j, y), v(x[0], x[1] + a // 16, x[1] + e // 16)) for y in range(16)]
 
     OWN = (0, 512, 1536)
-    SLT = ("SL", "S1", "S2")
+    H0, H1 = (0, 256), (256, 512)
+    PM = {p[0]: b for p, b in zip(MV, ("pM", "pC", "pM"))}
+    PN = {p[0]: b for p, b in zip(MV, ("pN", "pK1", "pN"))}
 
-    def goal_a(t, a, e):
-        tt(v("AG", a, e), ind(v("T1"), v(SLT[t], a // 16, e // 16)), v("CI", a, e) if t else v("bR", a, e), A.add)
+    def lists(t, j, a, e):
+        return v("L%d" % t, 32 * j + a // 16, 32 * j + e // 16)
 
-    def goal(t, a, e):
-        goal_a(t, a, e)
-        if t == 0:
-            tt(v("XG", a, e), ind(v("FB", 0, 512), v("FL", a // 16, e // 16)), v("AG", a, e), A.max)
+    def came(t):
+        return v("RW", 1024 * t - 1024, 1024 * t) if t else v("FB", 0, 512)
+
+    def ghost(t, a, e):
+        return v("FB", OWN[t] + 512 + a, OWN[t] + 512 + e) if t else v("Fg", a, e)
+
+    def goal_s(t, a, e):
+        p = "pA%d" % (a // 256)
+        act(v("Ts", a, e), ind(v("T12", 0, 1024), lists(t, 0, a, e)), F.Copy)
+        mm([(v(p, a, e), v("If"), v("Ts", a, e))] + spread(p, 0, ("IH", 32 if t else 64), a, e))
+
+    def goal_f(t, a, e):
+        act(ghost(t, a, e), ind(came(t), lists(t, 1, a, e)), F.Copy)
+
+    def clause_s():
+        act(v("Tc"), ind(v("T12"), v("CL")), F.Copy)
+
+    def clause_t(t):
+        mm([(v("pC"), v("If"), v("Tc"))] + spread("pC", 0, ("nw", 96) if t else ("IH", 0)))
+
+    def offs(t, a, e, s, on_v):
+        ts(v("P" + s, a, e), v("X" + s, a, e), 11, A.arith_shift_right, 2047, A.bitwise_and)
+        ts(v("Q" + s, a, e), v("X" + s, a, e), 2047, A.bitwise_and)
+        tt(v("PR" + s, a, e), v("P" + s, a, e), v("Q" + s, a, e), A.mult)
+        ts(v("OI" + s, a, e), v("PR" + s, a, e), 4, A.arith_shift_right, 8191, A.bitwise_and)
+        (cp if on_v else conv)(v("O" + s, a, e), v("OI" + s, a, e))
+        for j in range(a // 128, e // 128):
+            for q, n in enumerate("PQ"):
+                move(flat(j, q + 2 * (s == "C")), v(n + s, 128 * j, 128 * j + 128), "fl%d" % j, 64 * (t + 1))
+
+    def goal(t, a, e, on_v=False):
+        if t and a == 0:
+            tt(v("AG"), ind(v("T12", 0, 1024), lists(t, 0, a, e)), v("CI"), A.add)
+            tt(v("XG", a, e), ind(came(t), lists(t, 1, a, e)), v("AG"), A.max)
         else:
-            o = OWN[t] + 512
-            tt(v("XG", a, e), v("FB", o + a, o + e), v("AG", a, e), A.max)
-        offs(a, e, "XG", "PG", "QG", "OG")
+            tt(v("XG", a, e), ghost(t, a, e), v("pA%d" % (a // 256), a, e), A.max)
+        offs(t, a, e, "G", on_v)
 
-    def clause_a(t, a, e):
-        tt(v("AC", a, e), ind(v("T1"), v("CL", a // 16, e // 16)), v("bR", a, e) if t else v("CB", a, e), A.add)
-
-    def clause(t, a, e):
-        if t == 0:
-            clause_a(t, a, e)
-            tt(v("XC", a, e), v("FB", a, e), v("AC", a, e), A.max)
-        else:
-            tt(v("XC", a, e), ind(v("FB", OWN[t], OWN[t] + 1024), v("HL", a // 16, e // 16)), v("AC", a, e), A.max)
-        offs(a, e, "XC", "PC", "QC", "OC")
-        ts(v("nfr", a, e), v("XC", a, e), float(-(1 << 23)), A.not_equal)
-
-    def prep_mm(a, e):
-        mm([(v("p6", a, e), [(IM(3), v("nfr", a, e))])])
-
-    def own_prep(t, a, e):
-        p = v("p6", a, e)
+    def clause_e(a, e):
         ts(v("EG", a, e), v("XG", a, e), (1 << 22) - 1, A.bitwise_and)
-        tt(p, v("EG", a, e), p, A.add)
-        tt(v("cand", a, e), v("FB", OWN[t] + a, OWN[t] + e), p, A.max)
+
+    def clause(t, a, e, on_v=False):
+        if t == 0:
+            tt(v("pC", a, e), v("EG", a, e), v("pC", a, e), A.max)
+            tt(v("XC", a, e), v("FB", a, e), v("pC", a, e), A.max)
+        else:
+            tt(v("A2", a, e), v("EG", a, e), v("pC", a, e), A.max)
+            tt(v("XC", a, e), ind(v("FB", OWN[t], OWN[t] + 1024), v("HL", a // 16, e // 16)), v("A2", a, e), A.max)
+        offs(t, a, e, "C", on_v)
+
+    def free_rows(a, e):
+        act(v("sgf", a, e), v("XC", a, e), F.Sign, 0.5 - (1 << 22))
+
+    def bind_prep(t):
+        if t < 2:
+            conv(v("EF"), v("EG"))
+            a, e = MV[0]
+            mm([(v("pM", a, e), RC(0), v("row", a, e, 1, 1)), (v("pM", a, e), v("If"), v("EF", a, e))], True, False)
+        else:
+            conv(v("PH"), v("PG"))
+            conv(v("QH"), v("QG"))
+            mm([(v("pM"), RC(0), ONES), (v("pM"), IM(2048.0), v("PH")), (v("pM"), ONE, v("QH")), (v("pM"), ONE, v("QH"))], True, False)
+        if t:
+            keep_prep(0, MV[0][1] if t < 2 else 512)
+
+    def bind_free(t):
+        a, e = MV[0] if t < 2 else (0, 512)
+        mm([(v("pM", a, e), IM(float(-(1 << 23))), v("sgf", a, e))], False, False)
+        if t == 2:
+            conv(v("oi"), v("FB", OWN[2], OWN[2] + 512))
+
+    def keep_prep(a, e):
+        p = v(PN[a], a, e)
+        mm([(p, RC(1), v("row", a, e, 1, 1)), (p, IM(float(-(1 << 24))), v("mu", a, e))], True, False)
+
+    def kb(a, e):
+        return v("pK%d" % (a // 128 % 3), a, e)
 
     def grec(j):
         act(v("U", 2048 * j, 2048 * j + 2048), ind(v("xr"), v("OG", 128 * j, 128 * j + 128)), F.Copy)
 
-    def crec(j, lo=0, n=128):
-        a, e = 128 * j + lo, 128 * j + lo + n
-        tt(v("Df", 16 * a, 16 * e), ind(v("xr"), v("OC", a, e)), v("U", 16 * a, 16 * e), A.subtract)
+    def th_first(j):
+        p = kb(128 * j, 128 * j + 128)
+        mm([(p, ONE, v("OF")), (p, RC(3), v("row", 0, 128, 1, 1))], True, False)
 
-    def absd(j, lo=0, n=128):
-        a, e = 128 * j + lo, 128 * j + lo + n
-        act(v("Df", 16 * a, 16 * e), v("Df", 16 * a, 16 * e), F.Abs)
-        dsum(a, e)
+    def ksum(c, j, n):
+        a, e = 64 * c, 64 * c + 64
+        mm([(kb(a, e), Wq(j, r), v3(n, a, e, r)) for r in range(16)], False, c % 2 == 1 and j != 2)
 
-    def crec_s(j):
-        act(v("Df", 2048 * j, 2048 * j + 2048), ind(v("xr"), v("OC", 128 * j, 128 * j + 128)), F.Copy)
-        for m in range(4):
-            c = (2048 * j + 512 * m, 2048 * j + 512 * m + 512)
-            p = v("p7" if m % 2 else "p1")
-            mm([(p, [(ONE, v("Df", *c)), (IM(5), v("U", *c))])])
-            act(v("Df", *c), p, F.Abs)
-        dsum(128 * j, 128 * j + 128)
+    def crec_v(c):
+        for a in range(64 * c, 64 * c + 64, 16):
+            tt((T.D3[:, a // 16, :], [("D3", a, a + 16)], 256), ind(v("xr"), v("OC", a, a + 16)), v("U", 16 * a, 16 * a + 256), A.subtract)
+        ksum(c, 2, "D3")
 
-    def crec_r(j):
-        c = (2048 * j, 2048 * j + 2048)
-        crec(j)
-        ts(v("U", *c), v("Df", *c), 0.0, A.max, 2.0, A.mult)
-        a = 128 * j
-        mm([(v(dbank(a), a, a + 128),
-             [(v("VmN", 15 - k, 143 - k), v("Df", 16 * a + k, 16 * a + 2048, 16)) for k in range(16)]
-             + [(Wq(k), v("U", 16 * a + k, 16 * a + 2048, 16)) for k in range(16)] + [(IM(2), v("nfr", a, a + 128))])])
+    def relu_v(c):
+        ts(v3("R3", 64 * c, 64 * c + 64), v3("D3", 64 * c, 64 * c + 64), 0.0, A.max)
+        ksum(c, 1, "R3")
 
-    def dbank(a):
-        return "p0" if a < CH[0][1] else "p1" if a < CH[1][1] else "p7"
+    def crec_s(t, c, m):
+        p, w, u = v("pA%d" % m), 1024 * CS[t].index(c) + 512 * m, 1024 * c + 512 * m
+        act(v("W2", w, w + 512), ind(v("xr"), v("OC", 64 * c + 32 * m, 64 * c + 32 * m + 32)), F.Copy)
+        mm([(p, ONE, v("W2", w, w + 512)), (p, IM(-1.0), v("U", u, u + 512))])
 
-    def dsum(a, e):
-        mm([(v(dbank(a), a, e), [(Wq(k), v("Df", 16 * a + k, 16 * e, 16)) for k in range(16)] + [(IM(2), v("nfr", a, e))])])
+    def abs_s(c, m):
+        act(v3("D3", 64 * c + 32 * m, 64 * c + 32 * m + 32), v("pA%d" % m), F.Abs)
 
-    def keys(t, a, e):
-        D = v(dbank(a), a, e)
-        act(v("sgn", a, e), D, F.Sign, v("th2", 0, 1), -1.0)
-        act(v("Dc", a, e), D, F.Relu, -65536.0, 16.0)
-        mm([(v("p4", a, e), [(BO, v("sgn", a, e))] + ([(IM(10), v("a2", a, e))] if t else []))])
-        mm([(v("p2", m, m + 128), [(v("Dc", m, m + 128), v("If")), (R1, v("row", 0, 128, 1, 1)),
-                                   (v("sgn", m, m + 128), IM(1))]) for m in range(a, e, 128)])
+    def count(a, e):
+        tt(v("sg", a, e), kb(a, e), v("TK"), A.is_ge)
+        scan(v("Cn", a, e), v("sg", a, e), A.add)
 
-    def keys_b(t, a, e):
-        act(v("kS", a, e), v("p2", a, e), F.Copy)
-        act(v("sc", a, e), v("p4", a, e), F.Sign, -1.0 if t else 1.0, -1.0)
-        mm([(v("p4", a, e), [(IM(4), v("sc", a, e)), (R1, v("row", 1152 + a, 1152 + e, 1, 1))])])
+    def best(a, e):
+        tt(v("km", a, e), kb(a, e), v("sg", a, e), A.mult)
+        scan(v("Mn", a, e), v("km", a, e), A.min)
 
-    def best(t, a, e):
-        op("V", lambda: g.vector.tensor_tensor_scan(v("Mx", a, e)[0], v("seg", 0, e - a)[0], v("kS", a, e)[0], 0.0, A.mult, A.max),
-           [("seg", 0, 256), ("kS", a, e)], [("Mx", a, e)])
-        tt(v("oh", a, e), ind(v("Mx", a, e), v("Ex", 0, (e - a) // 16)), v("kS", a, e), A.is_equal)
-        mm([(v("p3", m, m + 128), [(v("oh", m, m + 128), ONE)]) for m in range(a, e, 128)])
+    def clash(t, n, f, a, e):
+        o, c = v(n, a // 16, e // 16), v("Cn", a + 15, e, 16)
+        if t:
+            tt(o, c, v("av", a // 16, e // 16), f)
+        else:
+            ts(o, c, 9.0, f)
 
-    def saves():
-        act(v("sg2"), v("Dc"), F.Sign, v("th2", 1, 2), -0.125)
-        mm([(v("p0", m, m + 128), [(v("oh", m, m + 128), ONE), (ONE, v("sg2", m, m + 128))]) for m in range(0, 512, 128)])
-        act(v("zb"), v("p0"), F.Relu, -1.0)
+    def pick(t, a, e, by):
+        c = (a // 16, e // 16)
+        tt(v("kf", *c), v("Mn", a + 15, e, 16), v("ncl", *c), A.mult)
+        ts(v("ko", *c), v("kf", *c), 4095, A.bitwise_and)
+        cp(v("ML", *c), v("ko", *c))
+        for j in range(a // 128, e // 128):
+            by(v("res", 128 * j, 128 * j + 128), ind(window(j), v("ML", 8 * j, 8 * j + 8)), F.Copy)
 
-    def zcol(a, e, j, n):
-        tt(v("Z", 512 * j + a, 512 * j + e), v(n, a, e), v("p3", a, e), A.mult)
+    def lsum(p, o, plane):
+        return [(v(p, o, o + 32), Wq(4 + plane, q), v("res", q, 512, 16)) for q in range(16)]
 
-    def lsum(p, o, n, a, e):
-        return (v(p, o, o + (e - a) // 16), [(Wq(q), v(n, a + q, e, 16)) for q in range(16)])
+    def chosen(p, o, plane):
+        mm(lsum(p, o, plane) + [(v(p, o, o + 32), IM(-16.0 if plane % 2 else -592.0), v("ncl")),
+                                (v(p, o, o + 32), ONE, v("Zc", 32 * plane, 32 * plane + 32))])
 
-    def choose_goal(t, a, e):
-        zcol(a, e, 1, "QG")
-        zcol(a, e, 0, "PG")
+    def on_clash(plane):
+        x = (v("ST", 0, 32), v("ST", 32, 64), v("NX"), v("IH", 0, 32))[plane]
+        tt(v("Zc", 32 * plane, 32 * plane + 32), x, v("cl"), A.mult)
 
-    def choose_clause(t, a, e):
-        zcol(a, e, 2, "PC")
-        zcol(a, e, 3, "QC")
+    def own_mm(t, a, e):
+        if a:
+            p = v(PM[a], a, e)
+            mm([(p, RC(0), v("row", a, e, 1, 1)), (p, v("If"), v("EF", a, e)), (p, IM(float(-(1 << 23))), v("sgf", a, e))], True, False)
+        if t:
+            if a:
+                keep_prep(a, e)
+            mm(spread(PN[a], 1, ("ncl", 0), a, e), False, True)
+        mm(spread(PM[a], 1, ("ncl", 0), a, e), False, True)
 
     def own_new(t, a, e):
-        p = v("p4", a, e)
-        tt(p, v("cand", a, e), p, A.add)
-        o = v("FB", OWN[t + 1] + a, OWN[t + 1] + e) if t < 2 else v("oi", a, e)
-        tt(o, v("keep", a, e) if t else v("FB", a, e), p, A.max)
-
-    def marks(t, a, e):
-        prs = [(IM(5), v("nfr", a, e)), (NBO, v("zb", a, e)), (IM(5), v("sc", a, e))]
         if t:
-            prs.append((ONE, v("mu", a, e)))
-        mm([(v("p4", a, e), prs)])
-        act(v("p4" if t == 2 else "mu", a, e), v("p4", a, e), F.Relu)
-        if t == 2:
-            act(v("p4", a, e), v("p4", a, e), F.Copy, -1.0)
-
-    LAST = ("S", "S", "H")
-
-    def lists_goal(t):
-        c2, d, G2 = v("cl2"), v("dd"), v("p5", 0, 64)
-        ts(v("cl2", 0, 32), v("p5", 128, 160), 0.0, A.is_gt)
-        ts(v("cl2", 32, 64), v("p5", 128, 160), 0.0, A.is_gt)
-        tt(d, v("SF0"), G2, A.subtract)
-        tt(d, d, c2, A.mult)
-        tt(v(LAST[t] + "F"), d, G2, A.add)
+            tt(v("keep", a, e), v("FB", OWN[t] + a, OWN[t] + e) if t < 2 else v("yv", a, e), v(PN[a], a, e), A.min)
+        o = v("FB", OWN[t + 1] + a, OWN[t + 1] + e) if t < 2 else v("yv", a, e)
+        tt(o, v("keep", a, e) if t else v("FB", a, e), v(PM[a], a, e), A.max)
         if t < 2:
-            ts(v("SL"), v("SF", 0, 32), -592.0, A.add)
-            ts(v("fxi"), v("SF", 32, 64), 496.0, A.add)
-            ts(v("fxi"), v("fxi"), 1023, A.bitwise_and)
-            cp(v("FL"), v("fxi"))
-
-    def lists_clause(t):
-        d, ch, c2, m = v("cz"), v("CHd" if t < 2 else "HC"), v("cl2"), v("m1")
-        ts(d, v("p6", 0, 64), 0.0, A.is_equal)
-        tt(d, d, v("p5", 0, 64), A.mult)
-        tt(v("CM"), d, v("p6", 0, 64), A.add)
-        tt(d, v("NXH"), v("CM"), A.subtract)
-        tt(d, d, c2, A.mult)
-        tt(ch, d, v("CM"), A.add)
-        if t < 2:
-            ts(v("CL"), v("CHd", 0, 32), -592.0, A.add)
-            ts(v("hb"), v("CHd", 32, 64), -16.0, A.add)
-            tt(m, v("CHd", 32, 64), v("IL"), A.is_equal)
-            ts(v("eqb"), m, float(-(1 << 23)), A.mult)
-            ts(v("HL"), v("CHd", 32, 64), -16.0, A.add)
-
-    def lists_save(t):
-        q, c2 = v("tq"), v("cl2")
-        tt(v("zz"), v("p6", 64, 128), c2, A.is_gt)
-        tt(q, v(LAST[t] + "F"), v("SF0"), A.subtract)
-        tt(q, q, v("zz"), A.mult)
-        tt(v(LAST[t] + "F0"), v("SF0"), q, A.add)
-
-    def save_c0(t):
-        m = v("m1")
-        tt(m, v("zz", 0, 32), v("cl2", 0, 32), A.add)
-        tt(v("tq", 0, 32), v("CHd" if t < 2 else "HC", 0, 32), v("CP0"), A.subtract)
-        tt(m, m, v("tq", 0, 32), A.mult)
-        tt(v("CP0" if t < 2 else "HC0"), v("CP0"), m, A.add)
+            b = MV.index((a, e))
+            send(t, v("RW", 1024 * t + a, 1024 * t + e), o, "ac%d%d" % (t, b), "lc%d%d" % (t, b))
 
     def next_clash():
-        n, s, i = v("nx", 0, 32), v("nx", 32, 64), v("nxi")
-        ts(n, v("CP0"), -592.0, A.add)
-        ts(s, v("SF0", 0, 32), -592.0, A.add)
-        tt(i, n, s, A.mult)
-        ts(i, i, 5, A.arith_shift_right)
-        ts(n, n, 1.0, A.add)
-        tt(i, i, n, A.add)
-        ts(i, i, 1023, A.bitwise_and)
-        ts(v("NXH", 0, 32), i, 592.0, A.add)
+        ts(v("n1"), v("ST", 0, 32), 32.0, A.add)
+        tt(v("n2"), v("n1"), v("ST", 64, 96), A.mult)
+        ts(v("n2"), v("n2"), 32.0, A.add)
+        ts(v("NX"), v("n2"), 5, A.arith_shift_right, 1023, A.bitwise_and)
+
+    def half_th():
+        mm(lsum("pK2", 0, 4) + [(v("pK2", 0, 32), IM(float(-(1 << 24))), v("cl"))])
+
+    def clause_lists():
+        tt(v("eq"), v("nw", 96, 128), v("IH", 0, 32), A.is_equal)
+        mm([(v("pA1", 0, 32), ONE, v("nw", 64, 96)), (v("pA1", 0, 32), IM(1024.0), v("eq"))])
+        cp(v("HL"), v("pK0", 32, 64))
+        cp(v("CL"), v("pA1", 0, 32))
+
+    def saves():
+        tt(v("ncs"), v("Mn", 15, 512, 16), v("pK2", 0, 32), A.is_lt)
+        p = v("pK1", 0, 96)
+        mm([(p, RC(2), v("row", 0, 96, 1, 1)), (p, ONE, v("nw", 0, 96))]
+           + [(v("pK1", 32 * j, 32 * j + 32), IM(-8192.0), v("ncs")) for j in range(3)])
+
+    def saved():
+        tt(v("SI"), v("ST"), v("pK1", 0, 96), A.max)
+        ts(v("ST"), v("SI"), 4095, A.bitwise_and)
+
+    def marks(t):
+        p = v("pN")
+        mm([(p, IM(float(-(1 << 23))), v("sgf"))] + ([(p, IM(float(1 << 24)), v("mu"))] if t else []), True, False)
+        mm(spread("pN", 1, ("ncs", 0)), False, True)
+        act(p if t == 2 else v("mu"), p, F.Relu, -0.5, 1.0 / (1 << 24))
+
+    def parity_mm():
+        mm([(v("pM", 0, 32), W16, v("cl"))])
+
+    def parity():
+        cp(v("ai"), v("pM", 0, 32))
+        ts(v("ai"), v("ai"), 1, A.bitwise_and)
+        ts(v("av"), v("ai"), -1.0, A.mult, 9.0, A.add)
 
     def send(t, dst_view, src_view, rs, ls):
+        calls.append(("G", lambda: send_now(t, dst_view, src_view, rs, ls), src_view[1], dst_view[1], 600, 3 * size(src_view)))
+
+    def send_now(t, dst_view, src_view, rs, ls):
         dst = T.cores[(rank + t + 1) % len(T.cores)]
         rid, pid, _ = topo.addr(dst)
         k = len(topo.engines(core, dst))
@@ -442,113 +573,115 @@ def rank_program(g, core, T, topo):
         cnt[rs] = len(topo.engines(src, core))
         note(rs, (rs, cnt[rs], {}), [], dst_view[1])
 
-    def number_out(j, p, hi, lo):
-        mm([(v(p, y, 512, 16, 8), [(v("Ib", y, 128, 16), lo)] + ([(v("Ib", 896 + y, 1024, 16), hi)] if hi else []))
-            for y in range(16)])
-        act(v("OUT", 512 * j, 512 * j + 512, 1, 8), v(p, 0, 512, 1, 8), F.Copy, float(-592 * 1024 - 16) if hi else -592.0)
-        store(T[("yg", "yc", "ysg", "yk")[j]][:], v("OUT", 512 * j, 512 * j + 512, 1, 8))
+    def packed(o, plane):
+        p = v("pA0", o, o + 32)
+        mm([(p, Wq(9 + plane // 2, q), v("res", q, 512, 16)) for q in range(16)]
+           + [(p, IM(-592.0 * 1024), v("ncl")), (p, IM(-16.0), v("ncl")), (p, IM(1024.0), v("Zc", 32 * plane, 32 * plane + 32)),
+              (p, ONE, v("Zc", 32 * plane + 32, 32 * plane + 64))])
 
-    def frames_out(a, e):
-        y = v("yv", a, e)
-        ts(v("lo", a, e), v("oi", a, e), 2047, A.bitwise_and)
-        tt(y, v("oi", a, e), v("lo", a, e), A.add)
-        act(y, y, F.Relu, v("th2", 4, 5))
+    def frames_old():
+        ts(v("lo"), v("oi"), 2047, A.bitwise_and)
+        tt(v("yv"), v("oi"), v("lo"), A.add)
+        ts(v("LF", 0, 32), v("ST", 0, 32), 1024.0, A.mult)
+        cp(v("LF", 32, 64), v("ST", 64, 96))
+        tt(v("LF", 0, 32), v("LF", 0, 32), v("ST", 32, 64), A.add)
 
-    def frames_end(a, e):
-        tt(v("yr", a, e), v("yv", a, e), v("p4", a, e), A.add)
-        store(T.yf[:, a:e], v("yr", a, e))
-
-    H0, H1 = (0, 256), (256, 512)
     for t in range(3):
-        for j in range(2):
-            goal(t, 128 * j, 128 * j + 128)
-            grec(j)
-            if t + j == 0:
-                clauses()
         if t == 0:
-            constants_a()
-        if t:
-            lists_save(t - 1)
-            save_c0(t - 1)
-            for c in (H0, H1):
-                clause_a(t, *c)
-        clause(t, *H0)
-        prep_mm(*H0)
-        crec_s(0)
-        goal(t, *H1)
-        grec(2)
-        own_prep(t, *H0)
-        clause(t, *H1)
-        prep_mm(*H1)
-        crec_r(1)
-        grec(3)
+            goal_s(t, *H0)
+            goal_f(t, *H0)
+            tables_b()
+            clause_s()
+            clause_t(t)
+        else:
+            goal_s(t, 128, 256)
+            goal_f(t, *H0)
+        goal_s(t, *H1)
+        goal_f(t, *H1)
+        goal(t, 0, 128, True)
         if t == 0:
-            constants_b()
-        keys(t, *CH[0])
-        crec(2)
-        absd(2)
-        crec(3, 0, 64)
-        keys_b(t, *CH[0])
-        crec(3, 64, 64)
-        absd(3, 0, 64)
-        if t:
-            tt(v("keep"), v("FB", OWN[t], OWN[t] + 512), v("p3"), A.min)
-        best(t, *CH[0])
-        keys(t, *CH[1])
-        absd(3, 64, 64)
-        own_prep(t, *H1)
-        choose_goal(t, *CH[0])
-        own_new(t, *CH[0])
-        keys_b(t, *CH[1])
-        keys(t, *CH[2])
-        best(t, *CH[1])
-        next_clash()
-        keys_b(t, *CH[2])
-        choose_goal(t, *CH[1])
-        mm([lsum("p5", 128, "sc", 0, 512)])
+            constants_v()
+            constants_s()
+            next_clash()
+        grec(0)
+        goal(t, 128, 256, t == 0)
+        goal(t, *H1, t == 0)
+        for h in (H0, H1):
+            clause_e(*h)
+            clause(t, *h, t == 0)
+        if t < 2:
+            send(t, v("RW", 1024 * t + 512, 1024 * t + 1024), v("FB", 1024 * t, 1024 * t + 512), "ag%d" % t, "lg%d" % t)
+        bind_prep(t)
+        free_rows(0, 512)
+        bind_free(t)
         if t == 2:
-            frames_out(*CH[0])
-        best(t, *CH[2])
-        own_new(t, *CH[1])
-        choose_goal(t, *CH[2])
-        mm([lsum("p5", 0, "Z", 0, 1024)])
-        own_new(t, *CH[2])
-        lists_goal(t)
+            frames_old()
+        for j in range(4):
+            if j:
+                grec(j)
+            th_first(j)
+            for c in (2 * j, 2 * j + 1):
+                if c in CS[t]:
+                    for m in range(2):
+                        crec_s(t, c, m)
+                        abs_s(c, m)
+                    ksum(c, 3, "D3")
+                else:
+                    crec_v(c)
+                    relu_v(c)
+            count(128 * j, 128 * j + 128)
+            best(128 * j, 128 * j + 128)
+        for p in MV:
+            clash(t, "ncl", A.is_ge, *p)
+            pick(t, *p, act if p[0] == 0 else cp)
+            if t < 2:
+                own_mm(t, *p)
+                own_new(t, *p)
+        clash(t, "cl", A.is_lt, 0, 512)
+        for plane in range(4):
+            on_clash(plane)
+        if t == 2:
+            break
+        chosen("pA0", 0, 0)
+        chosen("pA0", 32, 1)
+        cp(v("LS"), v("pA0", 0, 64))
+        send(t, v("L%d" % (t + 1)), v("LS"), "as%d" % t, "ls%d" % t)
+        chosen("pK0", 0, 2)
+        chosen("pK0", 32, 3)
+        parity_mm()
+        act(v("nw", 0, 64), v("pA0", 0, 64), F.Copy)
+        act(v("nw", 64, 128), v("pK0", 0, 64), F.Copy)
+        half_th()
+        clause_lists()
+        parity()
         saves()
-        if t < 2:
-            send(t, v(SLT[t + 1]), v("SL"), "as%d" % t, "ls%d" % t)
-            first = (0, 1024)[t]
-            o = OWN[t + 1] + 512
-            for b, (a, e) in enumerate(MV):
-                cp(v("col", a, e), ind(v("FB", first, first + 1024), v("FL", a // 16, e // 16)))
-                send(t, v("FB", o + a, o + e), v("col", a, e), "ac%d%d" % (t, b), "lc%d%d" % (t, b))
-        else:
-            number_out(0, "p1", v("HF", 0, 32), v("HF", 32, 64))
-        choose_clause(t, 0, 512)
-        mm([lsum("p6", 0, "Z", 1024, 2048)])
-        if t < 2:
-            mm([(v("p7"), [(ONES, v("sc"))])])
-            act(v("ab"), v("p7"), F.Abs, 0.0, 1.0 / 32)
-            act(v("ab"), v("ab"), F.Abs, v("th2", 2, 3))
-            act(v("a2"), v("ab"), F.Abs, v("th2", 3, 4))
-        if t < 2:
-            marks(t, 0, 512)
-        else:
-            frames_out(*H1)
-        lists_clause(t)
-        if t < 2:
-            mm([(v("p1", y, 512, 16), [(v("BY", 128 * y, 128 * y + 128), v("hb")), (v("BY", 128 * y, 128 * y + 128), v("eqb"))]) for y in range(16)])
-            act(v("bR"), v("p1"), F.Copy)
-            mm([lsum("p6", 64, "zb", 0, 512), lsum("p6", 96, "zb", 0, 512)])
-            mm([(v("p3"), [(R1, v("row", 640, 1152, 1, 1)), (IM(6), v("mu"))])])
-    mm([lsum("p6", 64, "zb", 0, 512), lsum("p6", 96, "zb", 0, 512)])
-    number_out(1, "p7", v("HC", 0, 32), v("HC", 32, 64))
-    marks(2, 0, 512)
-    lists_save(2)
-    save_c0(2)
-    number_out(2, "p1", v("HF0", 0, 32), v("HF0", 32, 64))
-    number_out(3, "p2", None, v("HC0"))
-    frames_end(*H0)
-    frames_end(*H1)
+        marks(t)
+        clause_s()
+        clause_t(t + 1)
+        saved()
+        next_clash()
+    own_mm(2, 0, 512)
+    half_th()
+    own_new(2, 0, 512)
+    tt(v("ncs"), v("Mn", 15, 512, 16), v("pK2", 0, 32), A.is_lt)
+    marks(2)
+    ts(v("yv"), v("yv"), float(-(C0 + 16 + (1 << 23))), A.add, -1.0, A.max)
+    packed(32, 0)
+    chosen("pA0", 64, 2)
+    packed(0, 2)
+    for a, e in (H0, H1):
+        tt(v("yr", a, e), v("yv", a, e), v("pN", a, e), A.add)
+        store(T.yf[:, a:e], v("yr", a, e), "YS"[a > 0])
+    d = v("LL", 0, 64)
+    tt(d, v("pA0", 32, 96), v("LF", 0, 64), A.subtract)
+    turn(v("OUT", 0, 64), v("pA0", 0, 64))
+    for j in range(2):
+        tt(v("LL", 32 * j, 32 * j + 32), v("LL", 32 * j, 32 * j + 32), v("ncs"), A.mult)
+    tt(d, v("pA0", 32, 96), d, A.subtract)
+    turn(v("OUT", 64, 128), d)
+    for j, y in enumerate((T.yc, T.yg, T.ysg, T.yk)):
+        for h in range(2):
+            store(y[h:8:2, :], v("OUT", 32 * j + 16 * h, 32 * j + 16 * h + 16), "YS"[h])
+    issue_all()
     for s in cnt:
         g.wait_ge(T.sem[s], cnt[s])

@@ -7,7 +7,21 @@ CS = ((5, 7), (5, 7), (5, 7))
 MV = ((0, 256), (256, 384), (384, 512))
 TURNS = 3
 ORDER = {}
-GATHER, WAKE, FLY, RATE = 1.56, 80, 1800, 170
+CA = ((3,), (3,), (3,))
+LP = ((0, 384), (384, 512))
+NV = 2
+QP = "C"
+LAST = 1
+DIRECT = 128
+SOON = (0, 0, 0, 0)
+GP = ((0, 128), (128, 256), (256, 384), (384, 512))
+UP = ((0, 128), (128, 256), (256, 384), (384, 512))
+ZERO = "GGDD"
+ON_V = 256
+ON_C = 0
+RES = (1, 1, 1)
+COST = (1.56, 120, 1600, 330, 4, 18)
+GATHER, WAKE, FLY, RATE, FAR, FIXED = COST
 
 
 def _sb(names, shape, d):
@@ -17,8 +31,10 @@ def _sb(names, shape, d):
 SCRATCH = {"xr": ("sbuf", [128, 8192], "bfloat16"), "T12": ("sbuf", [128, 2048], "float32"), "FB": ("sbuf", [128, 2560], "float32"),
            "RW": ("sbuf", [128, 2048], "float32"), "CI": ("sbuf", [128, 128], "int32"), "AG": ("sbuf", [128, 128], "float32"),
            "FLAT": ("sbuf", [128, 4 * FW], "int32"), "U": ("sbuf", [128, 8192], "bfloat16"), "W2": ("sbuf", [128, 3072], "bfloat16"),
-           "D3": ("sbuf", [128, 32, 256], "bfloat16"), "R3": ("sbuf", [128, 32, 256], "bfloat16"),
-           "Ib": ("sbuf", [128, 15 * 128], "bfloat16"), "BO": ("sbuf", [128, 256], "bfloat16"), "BY": ("sbuf", [128, 4096], "bfloat16"),
+           "D3": ("sbuf", [128, 32 // NV, 256 * NV], "bfloat16"), "R3": ("sbuf", [128, 32 // NV, 256 * NV], "bfloat16"),
+           "OIG": ("sbuf", [128, 32 // NV, 16 * NV], "int32"), "OIC": ("sbuf", [128, 32 // NV, 16 * NV], "int32"),
+           "Ib": ("sbuf", [128, 15 * 128], "bfloat16"), "BO": ("sbuf", [128, 256], "bfloat16"), "BY": ("sbuf", [128, 2048], "bfloat16"),
+           "B5": ("sbuf", [128, 128], "bfloat16"),
            "Vm": ("sbuf", [128, 11 * 144], "bfloat16"), "TH": ("sbuf", [128, 256], "bfloat16"), "OF": ("sbuf", [128, 128], "float16"),
            "TK": ("sbuf", [128, 128], "float32"), "row": ("sbuf", [128, 1024], "bfloat16"), "it": ("sbuf", [128, 512], "int32"), "il": ("sbuf", [128, 64], "int32"),
            "If": ("sbuf", [128, 128], "float32"), "seg": ("sbuf", [128, 128], "bfloat16"), "thi": ("sbuf", [128, 8], "int32"),
@@ -29,20 +45,21 @@ SCRATCH = {"xr": ("sbuf", [128, 8192], "bfloat16"), "T12": ("sbuf", [128, 2048],
            "nw": ("sbuf", [128, 128], "float16"), "Zc": ("sbuf", [128, 128], "float16"), "sv": ("sbuf", [128, 96], "float16"),
            "IH": ("sbuf", [128, 96], "float16"), "res": ("sbuf", [128, 512], "float16")}
 SCRATCH.update(_sb("Ts Tc Fg A2 EF keep Mn km yv yr", [128, 512], "float32"))
-SCRATCH.update(_sb("XG XC EG PG QG PC QC PRG PRC OIG OIC frb lo oi", [128, 512], "int32"))
+SCRATCH.update(_sb("XG XC EG PG QG PC QC PRG PRC frb lo oi", [128, 512], "int32"))
 SCRATCH.update(_sb("OG OC", [128, 512], "uint16"))
 SCRATCH.update(_sb("sgf mu sg Cn", [128, 512], "bfloat16"))
-SCRATCH.update(_sb("PH QH", [128, 512], "float16"))
+SCRATCH.update(_sb("PH QH QI cir", [128, 512], "float16"))
 SCRATCH.update(_sb("kf ko ai av NX n1 n2", [128, 32], "int32"))
 SCRATCH.update(_sb("cl ncl ncs eq", [128, 32], "bfloat16"))
-SCRATCH.update(_sb("CL HL ML", [128, 32], "uint16"))
+SCRATCH.update(_sb("CL HL ML NU", [128, 32], "uint16"))
+SCRATCH.update(_sb("CW", [128, 8], "float32"))
 SCRATCH.update(_sb("L0 L1 L2 LS", [128, 64], "uint16"))
 for _b in ("A0", "A1", "C", "K0", "K1", "K2", "M", "N"):
     SCRATCH["p" + _b] = ("psum", [128, 512], "float32")
 SEMAPHORES = ["sV", "sS", "sT", "sG"] + ["ld%d" % j for j in range(12)] + ["st%d" % j for j in range(12)]
-SEMAPHORES += ["fl%d" % j for j in range(4)] + ["h2"]
+SEMAPHORES += ["fl%d" % j for j in range(4)] + ["h2", "h3", "z1", "z2", "z3"]
 for _t in range(2):
-    SEMAPHORES += ["as%d" % _t, "ls%d" % _t, "ag%d" % _t, "lg%d" % _t] + ["%s%d%d" % (n, _t, b) for n in ("ac", "lc") for b in range(len(MV))]
+    SEMAPHORES += ["%s%d%d" % (n, _t, b) for n in ("as", "ls") for b in range(len(LP))] + ["ag%d" % _t, "lg%d" % _t] + ["%s%d%d" % (n, _t, b) for n in ("ac", "lc") for b in range(len(MV))]
 
 
 def rank_program(g, core, T, topo):
@@ -91,6 +108,7 @@ def rank_program(g, core, T, topo):
                     h[:] = [x for x in h if not (x[4] == e and not x[3] and a <= x[0] and x[1] <= b)]
                 h.append((a, b, tok, w, e))
 
+    soon = [0]
     calls = []
 
     def op(e, f, rd, wr, cyc, sem=None, upto=None, moved=0):
@@ -100,27 +118,30 @@ def rank_program(g, core, T, topo):
             cnt[s] = cnt.get(s, 0) + inc
             f().then_inc(T.sem[s], inc)
             note(e if sem is None else sem, (s, upto or cnt[s], dict(known[e])), rd, wr)
-        calls.append((e, issue, rd, wr, cyc, moved))
+        calls.append((e, issue, rd, wr, cyc, moved, soon[0]))
 
     def issue_all():
-        n = len(calls)
-        pre, seen = [set() for _ in calls], {}
-        for i, (e, f, rd, wr, cyc, moved) in enumerate(calls):
+        pre, seen, q, cyc, fly, what, more = [], {}, [], [], [], [], []
+        for e, f, rd, wr, c, moved, sooner in calls:
+            i = len(q)
+            more += [sooner] * (2 if moved else 1)
+            for step in ((e, c, FLY / 2, f), ("D", moved / RATE, FLY / 2, None)) if moved else ((e, c + FIXED * (e in "VS"), 0, f),):
+                for x, y in zip((q, cyc, fly, what, pre), step + ({i} if step[0] == "D" else set(),)):
+                    x.append(y)
             for regs, w in ((rd, 0), (wr, 1)):
                 for (x, a, b) in regs:
                     h = seen.setdefault(x, [])
                     if bank(x):
                         a, b, w = 0, 512, 1
-                    pre[i].update(j for (ha, hb, j, hw) in h if ha < b and a < hb and (w or hw) and j != i)
+                    pre[i].update(j for (ha, hb, j, hw) in h if ha < b and a < hb and (w or hw) and j < i)
                     if w:
                         h[:] = [y for y in h if not (a <= y[0] and y[1] <= b)]
-                    h.append((a, b, i, w))
-        post = [[] for _ in calls]
+                    h.append((a, b, len(q) - 1, w))
+        n = len(q)
+        post = [[] for _ in q]
         for i in range(n):
             for j in pre[i]:
                 post[j].append(i)
-        q, cyc = [c[0] for c in calls], [c[4] for c in calls]
-        fly = [FLY + c[5] / RATE if c[5] else 0 for c in calls]
 
         def plan(pre, post, rest, back):
             left, free, order, ends = [len(p) for p in pre], {e: 0.0 for e in "VSTGYD"}, [], [0.0] * n
@@ -133,33 +154,34 @@ def rank_program(g, core, T, topo):
                 i = max((j for j in todo if q[j] == e and max(ready[j], free[e]) < end), key=lambda j: rest[j] - max(ready[j] - free[e], 0))
                 todo.remove(i)
                 order.append(i)
-                free[e] = ends[i] = done = max(ready[i], free[e]) + cyc[i]
-                if fly[i] and not back:
-                    free["D"] = max(free["D"], done + FLY / 2) + fly[i] - FLY
-                    done = free["D"] + FLY / 2
+                free[e] = ends[i] = max(ready[i], free[e]) + cyc[i]
                 for j in post[i]:
-                    ready[j] = max(ready[j], done + (fly[j] if back else 0) + (0 if q[j] == e == "T" else WAKE))
+                    ready[j] = max(ready[j], ends[i] + fly[j if back else i] + (0 if q[j] == e == "T" else WAKE))
                     left[j] -= 1
                     if not left[j]:
                         todo.append(j)
             return max(ends[i] + (0 if back else fly[i]) for i in range(n)), order, ends
         ends, best = [200.0 * i for i in range(n)], ORDER.get(n)
         for turn in range(0 if best else TURNS):
-            rest = plan(post, pre, ends, True)[2]
-            now = plan(pre, post, [1e9 - 1e4 * i for i in range(nld[0])] + rest[nld[0]:], False)
+            rest = [x + y for x, y in zip(plan(post, pre, ends, True)[2], more)]
+            now = plan(pre, post, [1e9 - 1e4 * i for i in range(2 * nld[0])] + rest[2 * nld[0]:], False)
             ends = now[2]
             best = min(best or now, now)
         ORDER[n] = best
         for i in best[1]:
-            calls[i][1]()
+            if what[i]:
+                what[i]()
 
     def v(n, a=0, b=None, st=1, p=128):
         b = T[n].shape[1] if b is None else b
         return (T[n][0:p, a:b:st] if st > 1 else T[n][0:p, a:b], [(n, a, b)], (b - a + st - 1) // st)
 
     def v3(n, a, e, r=None):
-        c, d = a // 16, e // 16
-        return (T[n][:, c:d, :] if r is None else T[n][:, c:d, 16 * r:16 * r + 16], [(n, a, e)], (e - a) * (16 if r is None else 1))
+        w = 16 * NV
+        c, d = a // w, e // w
+        if e - a <= w and r is None:
+            return (T[n][:, c, 16 * (a % w):16 * (a % w + e - a)], [(n, a, e)], 16 * (e - a))
+        return (T[n][:, c:d, :] if r is None else T[n][:, c:d, w * r:w * r + w], [(n, a, e)], (e - a) * (16 if r is None else 1))
 
     def ind(win, off):
         return (win[0].indirect(off[0]), win[1] + off[1], None)
@@ -250,14 +272,22 @@ def rank_program(g, core, T, topo):
     iota(v("il", 0, 32), [[16, 32]], 0, 0)
     iota(v("il", 32, 33), [[0, 1]], 0, 1)
     iota(v("it", 256, 384), [[16, 8], [128, 16]], -1016, 0)
-    iota(v("CI"), [[1, 128]], 512, 0)
+    iota(v("CI"), [[1, 128]], 4096 + 512, 0)
 
     def window(j):
         return (T.FLAT[:, FW * j:FW * j + FW], [("FLAT%d" % q, j, j + 1) for q in range(6)], FW)
     for j in range(4):
-        iota(window(j), [[0, FW]], 0, 0)
-    SCALES = (1.0, None, -1.0, 2048.0, float(5 << 21), float(13 << 21), -592.0, -16.0, float(-(1 << 24)), float(1 << 23),
-              float(-(1 << 23)), float(1 << 24), -8192.0, 1024.0, -592.0 * 1024)
+        if ZERO[j] == "G":
+            iota(window(j), [[0, FW]], 0, 0)
+        elif ZERO[j] == "V":
+            op("V", lambda j=j: g.vector.memset(window(j)[0], 0), [], window(j)[1], FW)
+        else:
+            op("Y", lambda j=j: g.sync.dma_start(window(j)[0], window(0)[0]), window(0)[1], window(j)[1], 100, "z%d" % j, None, 512 * FW)
+    SCALES = (1.0, None, 2048.0, float(-(5 << 20)), float(-(13 << 20)), -1.0, float(-(1 << 23)), -592.0, -16.0, float(-(1 << 24)),
+              -0.5, -8192.0, 1024.0, -592.0 * 1024)
+
+    def put(o, x, pattern, c):
+        op("G", lambda: g.affine_select(o[0], x[0], pattern, A.not_equal, c, 0, 1), x[1], o[1], 200 + 2 * o[2])
 
     def IM(c):
         j = SCALES.index(c)
@@ -271,29 +301,33 @@ def rank_program(g, core, T, topo):
     def Wq(j, q):
         return v("Vm", 144 * j + 15 - q, 144 * j + 143 - q)
 
-    def BY(j, y):
-        return v("BY", 2048 * j + 128 * y, 2048 * j + 128 * y + 128)
+    def BY(y):
+        return v("BY", 128 * y, 128 * y + 128)
     ts(ONE, v("it", 0, 128), 0, A.is_equal)
     ts(v("it", 0, 128), v("it", 0, 128), 15, A.bitwise_and)
     ts(W16, v("it", 0, 128), 0, A.is_equal)
     ts(v("M16"), v("it", 0, 16), 0, A.is_equal)
     ts(v("it", 128, 256), v("it", 128, 256), 4, A.arith_shift_right)
     ts(BO, v("it", 128, 256), 0, A.is_equal)
-    for c in SCALES[3:6]:
+    for c in SCALES[2:5]:
         act(IM(c), ONE, F.Copy, 0.0, c)
     act(v("If"), ONE, F.Copy)
     for y in range(16):
-        act(BY(0, y), BO, F.Identity, 0.0, v("M16", y, y + 1))
+        act(BY(y), BO, F.Identity, 0.0, v("M16", y, y + 1))
+    fill(v("row", 0, 512, 1, 1), 1.0)
+    for j, c in enumerate((float(-(1 << 24)), float(1 << 24), 4096.0, -3072.0)):
+        fill(RC(j), c)
     for j in range(2):
         c = (512 * j, 512 * j + 512)
         cp(v("skh", *c), v("skb", *c))
-        ts(v("skv", *c), v("skh", *c), 1024.0, A.is_lt)
-        mm([(v("pA%d" % j), IM(2048.0), v("skh", *c)), (v("pA%d" % j), IM(SCALES[4]), v("skv", *c))])
-        act(v("T12", *c), v("pA%d" % j), F.Copy, float(C0 + (1 << 21)))
+        act(v("skv", *c), v("skb", *c), F.Sign, -1023.5)
+        mm([(v("pA%d" % j), IM(2048.0), v("skh", *c)), (v("pA%d" % j), IM(SCALES[3]), v("skv", *c))])
+    act(v("T12", 0, 512), v("pA0"), F.Copy, float(C0 - 4096 + (7 << 20)))
+    ts(v("T12", 512, 1024), v("pA1"), float(C0 - 4096 + (7 << 20)), A.add)
     cp(v("LF"), v("LT"))
     turn(v("LL"), v("LF"))
     cp(v("L0"), v("LL", 0, 64))
-    cp(v("IH", 64, 96), v("LL", 32, 64))
+    cp(v("IH", 32, 64), v("LL", 32, 64))
     ts(v("lo"), v("frb"), -(1 << 31) + (1023 << 10), A.bitwise_and)
     ts(v("pK0"), v("frb"), float(C0 + (1 << 23)), A.add)
     tt(v("FB", 0, 512), v("lo"), v("pK0"), A.add)
@@ -304,21 +338,23 @@ def rank_program(g, core, T, topo):
     for j in range(2):
         c = (512 * j, 512 * j + 512)
         q = ("pM", "pN")[j]
-        mm([(v(q), IM(2048.0), v("skh", *c)), (v(q), IM(SCALES[5]), v("skv", *c))])
+        mm([(v(q), IM(2048.0), v("skh", *c)), (v(q), IM(SCALES[4]), v("skv", *c))])
 
     def tables_b():
         for j in range(2):
-            act(v("T12", 1024 + 512 * j, 1536 + 512 * j), v(("pM", "pN")[j]), F.Copy, float(C0 + (1 << 21) - (1 << 24)))
+            act(v("T12", 1024 + 512 * j, 1536 + 512 * j), v(("pM", "pN")[j]), F.Copy, float(C0 - 4096 - (1 << 20)))
 
     def constants_v():
         fill(v("Vm", 0, 144), 0.0)
         cp(v("Vm", 15, 143, 16), v("BO", 0, 128, 16))
         cp(v("ST"), v("LL"))
-        ts(v("IH", 32, 64), v("IH", 0, 32), 512.0, A.add)
+        iota(v("oi", 0, 512, 1, 1), [[1, 512]], 512, 0)
+        conv(v("cir", 0, 512, 1, 1), v("oi", 0, 512, 1, 1))
         ts(v("OF"), v("it", 256, 384), v("thf", 7, 8), A.add)
+        fill(v("CW"), 0.0)
+        fill(v("CW", 0, 1), float(-(1 << 25)))
         fill(v("seg"), 1.0)
         fill(v("seg", 0, 128, 16), 0.0)
-        fill(v("row", 0, 512, 1, 1), 1.0)
         ts(v("thi", 1, 2), v("thi", 0, 1), 4, A.arith_shift_right)
         ts(v("thi", 2, 3), v("thi", 0, 1), 15, A.bitwise_and)
         ts(v("thi", 3, 4), v("thi", 0, 1), 1.0, A.add)
@@ -329,8 +365,8 @@ def rank_program(g, core, T, topo):
             move(flat(j, 4), v("H2"), "h2", 64)
 
     def constants_s():
-        for c in SCALES[2:3] + SCALES[6:]:
-            act(IM(c), ONE, F.Copy, 0.0, c)
+        for c in SCALES[5:]:
+            put(IM(c), ONE, [[-1, 128]], c)
         for j, c in ((1, -8192.0), (2, 4096.0), (3, -4096.0)):
             act(v("Vm", 144 * j, 144 * j + 144), v("Vm", 0, 144), F.Copy, 0.0, c)
         for j in range(4):
@@ -344,13 +380,13 @@ def rank_program(g, core, T, topo):
         act(v("BO", 128, 256), BO, F.Copy, 0.0, 16.0)
         mm([(v("pK0", 0, 128), v("BO", 128, 256), v("TH", 0, 128)), (v("pK0", 0, 128), BO, v("TH", 128, 256))])
         act(v("TK"), v("pK0", 0, 128), F.Copy, -4096.0, -4096.0)
-        for j, c in enumerate((float(-(1 << 24)), float(1 << 24), 4096.0, -3072.0)):
-            act(RC(j), v("row", 0, 128, 1, 1), F.Copy, 0.0, c)
+        act(v("B5"), BY(5), F.Copy, 0.0, float(1 << 24))
+        iota(v("it", 384, 512), [[0, 128]], 1, 0)
         for j in range(4):
-            act(v("BY", 2048 + 512 * j, 2560 + 512 * j), v("BY", 512 * j, 512 * j + 512), F.Copy, 0.0, float(1 << 24))
+            move(flat(j, 5), v("it", 384, 512), "h3", 64)
 
-    def spread(p, j, x, a=0, e=512):
-        return [(v(p, a + y, e, 16), BY(j, y), v(x[0], x[1] + a // 16, x[1] + e // 16)) for y in range(16)]
+    def spread(p, x, a=0, e=512):
+        return [(v(p, a + y, e, 16), BY(y), v(x[0], x[1] + a // 16, x[1] + e // 16)) for y in range(16)]
 
     OWN = (0, 512, 1536)
     H0, H1 = (0, 256), (256, 512)
@@ -358,7 +394,9 @@ def rank_program(g, core, T, topo):
     PN = {p[0]: b for p, b in zip(MV, ("pN", "pK1", "pN"))}
 
     def lists(t, j, a, e):
-        return v("L%d" % t, 32 * j + a // 16, 32 * j + e // 16)
+        c, d = [p for p in (LP if t else ((0, 512),)) if p[0] <= a and e <= p[1]][0]
+        o = (2 * c + j * (d - c) - c) // 16
+        return v("L%d" % t, o + a // 16, o + e // 16)
 
     def came(t):
         return v("RW", 1024 * t - 1024, 1024 * t) if t else v("FB", 0, 512)
@@ -366,10 +404,15 @@ def rank_program(g, core, T, topo):
     def ghost(t, a, e):
         return v("FB", OWN[t] + 512 + a, OWN[t] + 512 + e) if t else v("Fg", a, e)
 
+    def ab(t, a):
+        return "pK1" if t and a >= 384 else "pA%d" % (a // 256)
+
     def goal_s(t, a, e):
-        p = "pA%d" % (a // 256)
+        p = ab(t, a)
+        mm([(v(p, a, e), RC(2), v("row", a, e, 1, 1))]
+           + ([(v(p, a, e), v("row", 0, 128, 1, 1), v("cir", a, e, 1, 1))] if t else spread(p, ("IH", 32), a, e)), True, False)
         act(v("Ts", a, e), ind(v("T12", 0, 1024), lists(t, 0, a, e)), F.Copy)
-        mm([(v(p, a, e), v("If"), v("Ts", a, e))] + spread(p, 0, ("IH", 32 if t else 64), a, e))
+        mm([(v(p, a, e), v("If"), v("Ts", a, e))], False, True)
 
     def goal_f(t, a, e):
         act(ghost(t, a, e), ind(came(t), lists(t, 1, a, e)), F.Copy)
@@ -378,24 +421,33 @@ def rank_program(g, core, T, topo):
         act(v("Tc"), ind(v("T12"), v("CL")), F.Copy)
 
     def clause_t(t):
-        mm([(v("pC"), v("If"), v("Tc"))] + spread("pC", 0, ("nw", 96) if t else ("IH", 0)))
+        mm([(v("pC"), RC(2), ONES)] + spread("pC", ("nw", 96) if t else ("IH", 0)), True, False)
+        mm([(v("pC"), v("If"), v("Tc"))], False, True)
 
     def offs(t, a, e, s, on_v):
         ts(v("P" + s, a, e), v("X" + s, a, e), 11, A.arith_shift_right, 2047, A.bitwise_and)
         ts(v("Q" + s, a, e), v("X" + s, a, e), 2047, A.bitwise_and)
-        tt(v("PR" + s, a, e), v("P" + s, a, e), v("Q" + s, a, e), A.mult)
-        ts(v("OI" + s, a, e), v("PR" + s, a, e), 4, A.arith_shift_right, 8191, A.bitwise_and)
-        (cp if on_v else conv)(v("O" + s, a, e), v("OI" + s, a, e))
+        if on_v or s not in QP:
+            tt(v("PR" + s, a, e), v("P" + s, a, e), v("Q" + s, a, e), A.mult)
+        else:
+            h, p = v("QH" if s == "G" else "QI", a, e), v("pK2" if s == "G" else "pK0", a, e)
+            conv(h, v("Q" + s, a, e))
+            mm([(p, ONE, h)])
+            tt(v("PR" + s, a, e), v("P" + s, a, e), p, A.mult)
+        c, d = a // (16 * NV), e // (16 * NV)
+        ts((T["OI" + s][:, c:d, :], [("OI" + s, a, e)], e - a), v("PR" + s, a, e), 4, A.arith_shift_right, 8191, A.bitwise_and)
+        for j in range(NV):
+            (cp if on_v else conv)(v("O" + s, a + j, e, NV), (T["OI" + s][:, c:d, 16 * j:16 * j + 16], [("OI" + s, a, e)], (e - a) // NV))
         for j in range(a // 128, e // 128):
             for q, n in enumerate("PQ"):
                 move(flat(j, q + 2 * (s == "C")), v(n + s, 128 * j, 128 * j + 128), "fl%d" % j, 64 * (t + 1))
 
     def goal(t, a, e, on_v=False):
-        if t and a == 0:
-            tt(v("AG"), ind(v("T12", 0, 1024), lists(t, 0, a, e)), v("CI"), A.add)
-            tt(v("XG", a, e), ind(came(t), lists(t, 1, a, e)), v("AG"), A.max)
+        if t and a < DIRECT:
+            tt(v("AG", a, e), ind(v("T12", 0, 1024), lists(t, 0, a, e)), v("CI", a, e), A.add)
+            tt(v("XG", a, e), ind(came(t), lists(t, 1, a, e)), v("AG", a, e), A.max)
         else:
-            tt(v("XG", a, e), ghost(t, a, e), v("pA%d" % (a // 256), a, e), A.max)
+            tt(v("XG", a, e), ghost(t, a, e), v(ab(t, a), a, e), A.max)
         offs(t, a, e, "G", on_v)
 
     def clause_e(a, e):
@@ -416,30 +468,30 @@ def rank_program(g, core, T, topo):
     def bind_prep(t):
         if t < 2:
             conv(v("EF"), v("EG"))
-            a, e = MV[0]
-            mm([(v("pM", a, e), RC(0), v("row", a, e, 1, 1)), (v("pM", a, e), v("If"), v("EF", a, e))], True, False)
         else:
             conv(v("PH"), v("PG"))
             conv(v("QH"), v("QG"))
-            mm([(v("pM"), RC(0), ONES), (v("pM"), IM(2048.0), v("PH")), (v("pM"), ONE, v("QH")), (v("pM"), ONE, v("QH"))], True, False)
+        bind_first(t, *MV[0])
         if t:
-            keep_prep(0, MV[0][1] if t < 2 else 512)
+            keep_prep(*MV[0])
 
-    def bind_free(t):
-        a, e = MV[0] if t < 2 else (0, 512)
-        mm([(v("pM", a, e), IM(float(-(1 << 23))), v("sgf", a, e))], False, False)
-        if t == 2:
-            conv(v("oi"), v("FB", OWN[2], OWN[2] + 512))
+    def bind_first(t, a, e):
+        p = v(PM[a], a, e)
+        mm([(p, RC(0), v("row", a, e, 1, 1))] + ([(p, v("If"), v("EF", a, e))] if t < 2 else
+           [(p, IM(2048.0), v("PH", a, e)), (p, ONE, v("QH", a, e)), (p, ONE, v("QH", a, e))]), True, False)
 
-    def keep_prep(a, e):
+    def bind_free(a, e):
+        mm([(v(PM[a], a, e), IM(float(-(1 << 23))), v("sgf", a, e))], False, False)
+
+    def keep_prep(a, e, stop=False):
         p = v(PN[a], a, e)
-        mm([(p, RC(1), v("row", a, e, 1, 1)), (p, IM(float(-(1 << 24))), v("mu", a, e))], True, False)
+        mm([(p, RC(1), v("row", a, e, 1, 1)), (p, IM(float(-(1 << 24))), v("mu", a, e))], True, stop)
 
     def kb(a, e):
         return v("pK%d" % (a // 128 % 3), a, e)
 
-    def grec(j):
-        act(v("U", 2048 * j, 2048 * j + 2048), ind(v("xr"), v("OG", 128 * j, 128 * j + 128)), F.Copy)
+    def grec(a, e):
+        act(v("U", 16 * a, 16 * e), ind(v("xr"), v("OG", a, e)), F.Copy)
 
     def th_first(j):
         p = kb(128 * j, 128 * j + 128)
@@ -450,11 +502,16 @@ def rank_program(g, core, T, topo):
         mm([(kb(a, e), Wq(j, r), v3(n, a, e, r)) for r in range(16)], False, c % 2 == 1 and j != 2)
 
     def crec_v(c):
-        for a in range(64 * c, 64 * c + 64, 16):
-            tt((T.D3[:, a // 16, :], [("D3", a, a + 16)], 256), ind(v("xr"), v("OC", a, a + 16)), v("U", 16 * a, 16 * a + 256), A.subtract)
-        ksum(c, 2, "D3")
+        for a in range(64 * c, 64 * c + 64, 16 * NV):
+            e = a + 16 * NV
+            tt(v3("D3", a, e), ind(v("xr"), v("OC", a, e)), v("U", 16 * a, 16 * e), A.subtract)
+
+    def abs_a(c):
+        act(v3("R3", 64 * c, 64 * c + 64), v3("D3", 64 * c, 64 * c + 64), F.Abs)
+        ksum(c, 3, "R3")
 
     def relu_v(c):
+        ksum(c, 2, "D3")
         ts(v3("R3", 64 * c, 64 * c + 64), v3("D3", 64 * c, 64 * c + 64), 0.0, A.max)
         ksum(c, 1, "R3")
 
@@ -489,26 +546,53 @@ def rank_program(g, core, T, topo):
         for j in range(a // 128, e // 128):
             by(v("res", 128 * j, 128 * j + 128), ind(window(j), v("ML", 8 * j, 8 * j + 8)), F.Copy)
 
-    def lsum(p, o, plane):
-        return [(v(p, o, o + 32), Wq(4 + plane, q), v("res", q, 512, 16)) for q in range(16)]
+    def lsum(p, o, plane, a=0, e=512):
+        return [(v(p, o, o + (e - a) // 16), Wq(4 + plane, q), v("res", a + q, e, 16)) for q in range(16)]
 
-    def chosen(p, o, plane):
-        mm(lsum(p, o, plane) + [(v(p, o, o + 32), IM(-16.0 if plane % 2 else -592.0), v("ncl")),
-                                (v(p, o, o + 32), ONE, v("Zc", 32 * plane, 32 * plane + 32))])
+    def chosen(p, o, plane, a=0, e=512):
+        c, d, out = a // 16, e // 16, v(p, o, o + (e - a) // 16)
+        mm(lsum(p, o, plane, a, e) + [(out, IM(-16.0 if plane % 2 else -592.0), v("ncl", c, d)),
+                                      (out, ONE, v("Zc", 32 * plane + c, 32 * plane + d))])
 
-    def on_clash(plane):
-        x = (v("ST", 0, 32), v("ST", 32, 64), v("NX"), v("IH", 0, 32))[plane]
-        tt(v("Zc", 32 * plane, 32 * plane + 32), x, v("cl"), A.mult)
+    def on_clash(plane, a=0, e=512):
+        x, o = (("ST", 0), ("ST", 32), ("NX", 0), ("IH", 0))[plane]
+        tt(v("Zc", 32 * plane + a // 16, 32 * plane + e // 16), v(x, o + a // 16, o + e // 16), v("cl", a // 16, e // 16), A.mult)
+
+    def goals_out(t, a, e):
+        c, n, b = a // 16, (e - a) // 16, LP.index((a, e))
+        for plane in range(2):
+            on_clash(plane, a, e)
+            chosen("pK2", plane * n, plane, a, e)
+        cp(v("LS", 2 * c, 2 * c + 2 * n), v("pK2", 0, 2 * n))
+        send(t, v("L%d" % (t + 1), 2 * c, 2 * c + 2 * n), v("LS", 2 * c, 2 * c + 2 * n), "as%d%d" % (t, b), "ls%d%d" % (t, b))
+        for plane in range(2):
+            act(v("nw", 32 * plane + c, 32 * plane + c + n), v("pK2", plane * n, plane * n + n), F.Copy)
+
+    def own_last(t, a, e):
+        p, f = v(PM[a], a, e), v("FB", OWN[t] + a, OWN[t] + e)
+        mm([(p, v("If"), v("EF", a, e)), (p, IM(float(-(1 << 23))), v("sgf", a, e))])
+        tt(v("A2", a, e), f, p, A.max)
+        if t:
+            keep_prep(a, e, True)
+            tt(v("keep", a, e), f, v(PN[a], a, e), A.min)
+            cp(v("NU", a // 16, e // 16), v("ncl", a // 16, e // 16))
+        else:
+            ts(v("NU", a // 16, e // 16), v("Cn", a + 15, e, 16), 9.0, A.is_ge)
+        tt(v("Ts", a, e), ind(v("CW"), v("NU", a // 16, e // 16)), v("A2", a, e), A.add)
+        o = v("FB", OWN[t + 1] + a, OWN[t + 1] + e)
+        tt(o, v("Ts", a, e), v("keep", a, e) if t else f, A.max)
+        b = MV.index((a, e))
+        send(t, v("RW", 1024 * t + a, 1024 * t + e), o, "ac%d%d" % (t, b), "lc%d%d" % (t, b))
 
     def own_mm(t, a, e):
         if a:
-            p = v(PM[a], a, e)
-            mm([(p, RC(0), v("row", a, e, 1, 1)), (p, v("If"), v("EF", a, e)), (p, IM(float(-(1 << 23))), v("sgf", a, e))], True, False)
+            bind_first(t, a, e)
+            bind_free(a, e)
         if t:
             if a:
                 keep_prep(a, e)
-            mm(spread(PN[a], 1, ("ncl", 0), a, e), False, True)
-        mm(spread(PM[a], 1, ("ncl", 0), a, e), False, True)
+            mm([(v(PN[a], a, e), v("B5"), v("res", a, e))], False, True)
+        mm([(v(PM[a], a, e), v("B5"), v("res", a, e))], False, True)
 
     def own_new(t, a, e):
         if t:
@@ -518,6 +602,8 @@ def rank_program(g, core, T, topo):
         if t < 2:
             b = MV.index((a, e))
             send(t, v("RW", 1024 * t + a, 1024 * t + e), o, "ac%d%d" % (t, b), "lc%d%d" % (t, b))
+        else:
+            ts(o, o, float(-(C0 + 16 + (1 << 23))), A.add, -1.0, A.max)
 
     def next_clash():
         ts(v("n1"), v("ST", 0, 32), 32.0, A.add)
@@ -526,16 +612,16 @@ def rank_program(g, core, T, topo):
         ts(v("NX"), v("n2"), 5, A.arith_shift_right, 1023, A.bitwise_and)
 
     def half_th():
-        mm(lsum("pK2", 0, 4) + [(v("pK2", 0, 32), IM(float(-(1 << 24))), v("cl"))])
+        mm(lsum("pK1", 96, 4) + [(v("pK1", 96, 128), IM(float(-(1 << 24))), v("cl"))])
+        tt(v("ncs"), v("Mn", 15, 512, 16), v("pK1", 96, 128), A.is_lt)
 
     def clause_lists():
         tt(v("eq"), v("nw", 96, 128), v("IH", 0, 32), A.is_equal)
-        mm([(v("pA1", 0, 32), ONE, v("nw", 64, 96)), (v("pA1", 0, 32), IM(1024.0), v("eq"))])
+        mm([(v("pM", 32, 64), ONE, v("nw", 64, 96)), (v("pM", 32, 64), IM(1024.0), v("eq"))])
         cp(v("HL"), v("pK0", 32, 64))
-        cp(v("CL"), v("pA1", 0, 32))
+        cp(v("CL"), v("pM", 32, 64))
 
     def saves():
-        tt(v("ncs"), v("Mn", 15, 512, 16), v("pK2", 0, 32), A.is_lt)
         p = v("pK1", 0, 96)
         mm([(p, RC(2), v("row", 0, 96, 1, 1)), (p, ONE, v("nw", 0, 96))]
            + [(v("pK1", 32 * j, 32 * j + 32), IM(-8192.0), v("ncs")) for j in range(3)])
@@ -545,10 +631,11 @@ def rank_program(g, core, T, topo):
         ts(v("ST"), v("SI"), 4095, A.bitwise_and)
 
     def marks(t):
-        p = v("pN")
-        mm([(p, IM(float(-(1 << 23))), v("sgf"))] + ([(p, IM(float(1 << 24)), v("mu"))] if t else []), True, False)
-        mm(spread("pN", 1, ("ncs", 0)), False, True)
-        act(p if t == 2 else v("mu"), p, F.Relu, -0.5, 1.0 / (1 << 24))
+        b = "pN" if t < 2 else "pC"
+        mm([(v(b), IM(-0.5), v("sgf"))] + ([(v(b), ONE, v("mu"))] if t else []), True, False)
+        mm(spread(b, ("ncs", 0)), False, True)
+        for h in ((0, 512),) if t < 2 else (H0, H1):
+            act(v("mu" if t < 2 else "pK2" if h[0] else "pK0", *h), v(b, *h), F.Relu, -0.5)
 
     def parity_mm():
         mm([(v("pM", 0, 32), W16, v("cl"))])
@@ -559,7 +646,8 @@ def rank_program(g, core, T, topo):
         ts(v("av"), v("ai"), -1.0, A.mult, 9.0, A.add)
 
     def send(t, dst_view, src_view, rs, ls):
-        calls.append(("G", lambda: send_now(t, dst_view, src_view, rs, ls), src_view[1], dst_view[1], 600, 3 * size(src_view)))
+        calls.append(("G", lambda: send_now(t, dst_view, src_view, rs, ls), src_view[1], dst_view[1],
+                      4000 if rs == "ag0" else 600, FAR * size(src_view), soon[0]))
 
     def send_now(t, dst_view, src_view, rs, ls):
         dst = T.cores[(rank + t + 1) % len(T.cores)]
@@ -573,15 +661,17 @@ def rank_program(g, core, T, topo):
         cnt[rs] = len(topo.engines(src, core))
         note(rs, (rs, cnt[rs], {}), [], dst_view[1])
 
-    def packed(o, plane):
-        p = v("pA0", o, o + 32)
+    def packed(b, plane):
+        p = v(b, 0, 32)
         mm([(p, Wq(9 + plane // 2, q), v("res", q, 512, 16)) for q in range(16)]
            + [(p, IM(-592.0 * 1024), v("ncl")), (p, IM(-16.0), v("ncl")), (p, IM(1024.0), v("Zc", 32 * plane, 32 * plane + 32)),
               (p, ONE, v("Zc", 32 * plane + 32, 32 * plane + 64))])
 
     def frames_old():
-        ts(v("lo"), v("oi"), 2047, A.bitwise_and)
-        tt(v("yv"), v("oi"), v("lo"), A.add)
+        for a, e in MV:
+            conv(v("oi", a, e), v("FB", OWN[2] + a, OWN[2] + e))
+            ts(v("lo", a, e), v("oi", a, e), 2047, A.bitwise_and)
+            tt(v("yv", a, e), v("oi", a, e), v("lo", a, e), A.add)
         ts(v("LF", 0, 32), v("ST", 0, 32), 1024.0, A.mult)
         cp(v("LF", 32, 64), v("ST", 64, 96))
         tt(v("LF", 0, 32), v("LF", 0, 32), v("ST", 32, 64), A.add)
@@ -594,31 +684,32 @@ def rank_program(g, core, T, topo):
             clause_s()
             clause_t(t)
         else:
-            goal_s(t, 128, 256)
+            goal_s(t, DIRECT, 256)
             goal_f(t, *H0)
-        goal_s(t, *H1)
-        goal_f(t, *H1)
-        goal(t, 0, 128, True)
+        for p in (H1,) if t == 0 else ((256, 384), (384, 512)):
+            goal_s(t, *p)
+            goal_f(t, *p)
         if t == 0:
             constants_v()
             constants_s()
             next_clash()
-        grec(0)
-        goal(t, 128, 256, t == 0)
-        goal(t, *H1, t == 0)
+        for a, e in GP:
+            goal(t, a, e, a == 0 or (t == 0 and a < ON_V))
         for h in (H0, H1):
             clause_e(*h)
-            clause(t, *h, t == 0)
+            clause(t, *h, t == 0 and h[0] < ON_C)
+        for p in UP:
+            grec(*p)
         if t < 2:
             send(t, v("RW", 1024 * t + 512, 1024 * t + 1024), v("FB", 1024 * t, 1024 * t + 512), "ag%d" % t, "lg%d" % t)
+        soon[0] = SOON[0]
         bind_prep(t)
         free_rows(0, 512)
-        bind_free(t)
+        bind_free(*MV[0])
+        soon[0] = 0
         if t == 2:
             frames_old()
         for j in range(4):
-            if j:
-                grec(j)
             th_first(j)
             for c in (2 * j, 2 * j + 1):
                 if c in CS[t]:
@@ -628,56 +719,61 @@ def rank_program(g, core, T, topo):
                     ksum(c, 3, "D3")
                 else:
                     crec_v(c)
-                    relu_v(c)
+                    (abs_a if c in CA[t] else relu_v)(c)
+            soon[0] = SOON[1]
             count(128 * j, 128 * j + 128)
             best(128 * j, 128 * j + 128)
-        for p in MV:
+            soon[0] = 0
+        soon[0] = SOON[2]
+        for b, p in enumerate(MV):
             clash(t, "ncl", A.is_ge, *p)
-            pick(t, *p, act if p[0] == 0 else cp)
-            if t < 2:
+            pick(t, *p, act if RES[b] else cp)
+            if t < 2 and p[1] == 512 and LAST:
+                own_last(t, *p)
+            else:
                 own_mm(t, *p)
                 own_new(t, *p)
-        clash(t, "cl", A.is_lt, 0, 512)
-        for plane in range(4):
-            on_clash(plane)
         if t == 2:
+            clash(t, "cl", A.is_lt, 0, 512)
+            for plane in range(4):
+                on_clash(plane)
             break
-        chosen("pA0", 0, 0)
-        chosen("pA0", 32, 1)
-        cp(v("LS"), v("pA0", 0, 64))
-        send(t, v("L%d" % (t + 1)), v("LS"), "as%d" % t, "ls%d" % t)
+        for p in LP:
+            clash(t, "cl", A.is_lt, *p)
+            goals_out(t, *p)
+        soon[0] = SOON[3]
+        on_clash(2)
+        on_clash(3)
         chosen("pK0", 0, 2)
         chosen("pK0", 32, 3)
         parity_mm()
-        act(v("nw", 0, 64), v("pA0", 0, 64), F.Copy)
+        parity()
         act(v("nw", 64, 128), v("pK0", 0, 64), F.Copy)
         half_th()
         clause_lists()
-        parity()
         saves()
         marks(t)
         clause_s()
         clause_t(t + 1)
         saved()
         next_clash()
-    own_mm(2, 0, 512)
+        soon[0] = 0
+    soon[0] = 0
     half_th()
-    own_new(2, 0, 512)
-    tt(v("ncs"), v("Mn", 15, 512, 16), v("pK2", 0, 32), A.is_lt)
     marks(2)
-    ts(v("yv"), v("yv"), float(-(C0 + 16 + (1 << 23))), A.add, -1.0, A.max)
-    packed(32, 0)
-    chosen("pA0", 64, 2)
-    packed(0, 2)
+    packed("pA0", 0)
+    chosen("pA0", 32, 2)
+    packed("pA1", 2)
     for a, e in (H0, H1):
-        tt(v("yr", a, e), v("yv", a, e), v("pN", a, e), A.add)
+        tt(v("yr", a, e), v("yv", a, e), v("pK2" if a else "pK0", a, e), A.add)
         store(T.yf[:, a:e], v("yr", a, e), "YS"[a > 0])
     d = v("LL", 0, 64)
-    tt(d, v("pA0", 32, 96), v("LF", 0, 64), A.subtract)
-    turn(v("OUT", 0, 64), v("pA0", 0, 64))
+    tt(d, v("pA0", 0, 64), v("LF", 0, 64), A.subtract)
+    turn(v("OUT", 32, 64), v("pA0", 0, 32))
+    turn(v("OUT", 0, 32), v("pA1", 0, 32))
     for j in range(2):
         tt(v("LL", 32 * j, 32 * j + 32), v("LL", 32 * j, 32 * j + 32), v("ncs"), A.mult)
-    tt(d, v("pA0", 32, 96), d, A.subtract)
+    tt(d, v("pA0", 0, 64), d, A.subtract)
     turn(v("OUT", 64, 128), d)
     for j, y in enumerate((T.yc, T.yg, T.ysg, T.yk)):
         for h in range(2):

from concourse.mybir import AluOpType, ActivationFunctionType
A = AluOpType
F = ActivationFunctionType
C0 = 592 * 2048 + 16
FW = 2056
CS = ((5, 7), (5, 7), (5, 7))
MV = ((0, 256), (256, 384), (384, 512))
TURNS = 3
ORDER = {}
CA = ((3,), (3,), (3,))
LP = ((0, 384), (384, 512))
NV = 2
QP = "C"
LAST = 1
DIRECT = 128
SOON = (0, 0, 0, 0)
GP = ((0, 128), (128, 256), (256, 384), (384, 512))
UP = ((0, 128), (128, 256), (256, 384), (384, 512))
ZERO = "GGDD"
ON_V = 256
ON_C = 0
RES = (1, 1, 1)
COST = (1.56, 120, 1600, 330, 4, 18)
GATHER, WAKE, FLY, RATE, FAR, FIXED = COST


def _sb(names, shape, d):
    return {n: ("sbuf", shape, d) for n in names.split()}


SCRATCH = {"xr": ("sbuf", [128, 8192], "bfloat16"), "T12": ("sbuf", [128, 2048], "float32"), "FB": ("sbuf", [128, 2560], "float32"),
           "RW": ("sbuf", [128, 2048], "float32"), "CI": ("sbuf", [128, 128], "int32"), "AG": ("sbuf", [128, 128], "float32"),
           "FLAT": ("sbuf", [128, 4 * FW], "int32"), "U": ("sbuf", [128, 8192], "bfloat16"), "W2": ("sbuf", [128, 3072], "bfloat16"),
           "D3": ("sbuf", [128, 32 // NV, 256 * NV], "bfloat16"), "R3": ("sbuf", [128, 32 // NV, 256 * NV], "bfloat16"),
           "OIG": ("sbuf", [128, 32 // NV, 16 * NV], "int32"), "OIC": ("sbuf", [128, 32 // NV, 16 * NV], "int32"),
           "Ib": ("sbuf", [128, 15 * 128], "bfloat16"), "BO": ("sbuf", [128, 256], "bfloat16"), "BY": ("sbuf", [128, 2048], "bfloat16"),
           "B5": ("sbuf", [128, 128], "bfloat16"),
           "Vm": ("sbuf", [128, 11 * 144], "bfloat16"), "TH": ("sbuf", [128, 256], "bfloat16"), "OF": ("sbuf", [128, 128], "float16"),
           "TK": ("sbuf", [128, 128], "float32"), "row": ("sbuf", [128, 1024], "bfloat16"), "it": ("sbuf", [128, 512], "int32"), "il": ("sbuf", [128, 64], "int32"),
           "If": ("sbuf", [128, 128], "float32"), "seg": ("sbuf", [128, 128], "bfloat16"), "thi": ("sbuf", [128, 8], "int32"),
           "thf": ("sbuf", [128, 8], "float32"), "M16": ("sbuf", [128, 16], "float32"), "H2": ("sbuf", [128, 128], "int32"),
           "skb": ("sbuf", [128, 1024], "int32"), "skh": ("sbuf", [128, 1024], "float16"), "skv": ("sbuf", [128, 1024], "bfloat16"),
           "LT": ("sbuf", [128, 96], "int32"), "ST": ("sbuf", [128, 96], "int32"), "SI": ("sbuf", [128, 96], "int32"),
           "LF": ("sbuf", [128, 96], "float32"), "LL": ("sbuf", [128, 96], "float32"), "OUT": ("sbuf", [128, 128], "float32"),
           "nw": ("sbuf", [128, 128], "float16"), "Zc": ("sbuf", [128, 128], "float16"), "sv": ("sbuf", [128, 96], "float16"),
           "IH": ("sbuf", [128, 96], "float16"), "res": ("sbuf", [128, 512], "float16")}
SCRATCH.update(_sb("Ts Tc Fg A2 EF keep Mn km yv yr", [128, 512], "float32"))
SCRATCH.update(_sb("XG XC EG PG QG PC QC PRG PRC frb lo oi", [128, 512], "int32"))
SCRATCH.update(_sb("OG OC", [128, 512], "uint16"))
SCRATCH.update(_sb("sgf mu sg Cn", [128, 512], "bfloat16"))
SCRATCH.update(_sb("PH QH QI cir", [128, 512], "float16"))
SCRATCH.update(_sb("kf ko ai av NX n1 n2", [128, 32], "int32"))
SCRATCH.update(_sb("cl ncl ncs eq", [128, 32], "bfloat16"))
SCRATCH.update(_sb("CL HL ML NU", [128, 32], "uint16"))
SCRATCH.update(_sb("CW", [128, 8], "float32"))
SCRATCH.update(_sb("L0 L1 L2 LS", [128, 64], "uint16"))
for _b in ("A0", "A1", "C", "K0", "K1", "K2", "M", "N"):
    SCRATCH["p" + _b] = ("psum", [128, 512], "float32")
SEMAPHORES = ["sV", "sS", "sT", "sG"] + ["ld%d" % j for j in range(12)] + ["st%d" % j for j in range(12)]
SEMAPHORES += ["fl%d" % j for j in range(4)] + ["h2", "h3", "z1", "z2", "z3"]
for _t in range(2):
    SEMAPHORES += ["%s%d%d" % (n, _t, b) for n in ("as", "ls") for b in range(len(LP))] + ["ag%d" % _t, "lg%d" % _t] + ["%s%d%d" % (n, _t, b) for n in ("ac", "lc") for b in range(len(MV))]


def rank_program(g, core, T, topo):
    rank = T.rank_of(core)
    if rank is None:
        return
    ENG = {"V": g.vector, "S": g.scalar, "T": g.tensor, "G": g, "Y": g.sync}
    known = {e: {} for e in ENG}
    cnt, hist = {}, {}

    def bank(n):
        return n[0] == "p" and n[1].isupper()

    def touch(e, rd, wr):
        toks = []
        for regs, w in ((rd, 0), (wr, 1)):
            for (n, a, b) in regs:
                for (ha, hb, tok, hw, he) in hist.get(n, []):
                    if he == e and e == "T":
                        continue
                    if bank(n):
                        if he != e or hw or w:
                            toks.append(tok)
                    elif ha < b and a < hb and (w or hw):
                        toks.append(tok)
        best = {}
        for tok in toks:
            if known[e].get(tok[0], 0) < tok[1] and (tok[0] not in best or best[tok[0]][1] < tok[1]):
                best[tok[0]] = tok
        todo = [t for t in best.values() if not any(o is not t and o[2].get(t[0], 0) >= t[1] for o in best.values())]
        for t in todo:
            ENG[e].wait_ge(T.sem[t[0]], t[1])
            for s, c in list(t[2].items()) + [(t[0], t[1])]:
                known[e][s] = max(known[e].get(s, 0), c)

    def note(e, tok, rd, wr):
        for regs, w in ((rd, 0), (wr, 1)):
            for (n, a, b) in regs:
                h = hist.setdefault(n, [])
                if bank(n):
                    h[:] = [(0, 512, tok, any(x[3] for x in h if x[4] == e) or w, e)]
                    continue
                if w:
                    h[:] = [x for x in h if not (a <= x[0] and x[1] <= b)]
                else:
                    h[:] = [x for x in h if not (x[4] == e and not x[3] and a <= x[0] and x[1] <= b)]
                h.append((a, b, tok, w, e))

    soon = [0]
    calls = []

    def op(e, f, rd, wr, cyc, sem=None, upto=None, moved=0):
        def issue():
            touch(e, rd, wr)
            s, inc = sem or "s" + e, 16 if sem else 1
            cnt[s] = cnt.get(s, 0) + inc
            f().then_inc(T.sem[s], inc)
            note(e if sem is None else sem, (s, upto or cnt[s], dict(known[e])), rd, wr)
        calls.append((e, issue, rd, wr, cyc, moved, soon[0]))

    def issue_all():
        pre, seen, q, cyc, fly, what, more = [], {}, [], [], [], [], []
        for e, f, rd, wr, c, moved, sooner in calls:
            i = len(q)
            more += [sooner] * (2 if moved else 1)
            for step in ((e, c, FLY / 2, f), ("D", moved / RATE, FLY / 2, None)) if moved else ((e, c + FIXED * (e in "VS"), 0, f),):
                for x, y in zip((q, cyc, fly, what, pre), step + ({i} if step[0] == "D" else set(),)):
                    x.append(y)
            for regs, w in ((rd, 0), (wr, 1)):
                for (x, a, b) in regs:
                    h = seen.setdefault(x, [])
                    if bank(x):
                        a, b, w = 0, 512, 1
                    pre[i].update(j for (ha, hb, j, hw) in h if ha < b and a < hb and (w or hw) and j < i)
                    if w:
                        h[:] = [y for y in h if not (a <= y[0] and y[1] <= b)]
                    h.append((a, b, len(q) - 1, w))
        n = len(q)
        post = [[] for _ in q]
        for i in range(n):
            for j in pre[i]:
                post[j].append(i)

        def plan(pre, post, rest, back):
            left, free, order, ends = [len(p) for p in pre], {e: 0.0 for e in "VSTGYD"}, [], [0.0] * n
            ready = [fly[i] if back else 0.0 for i in range(n)]
            todo = [i for i in range(n) if not left[i]]
            while todo:
                first = min(todo, key=lambda i: max(ready[i], free[q[i]]) + cyc[i])
                e = q[first]
                end = max(ready[first], free[e]) + cyc[first]
                i = max((j for j in todo if q[j] == e and max(ready[j], free[e]) < end), key=lambda j: rest[j] - max(ready[j] - free[e], 0))
                todo.remove(i)
                order.append(i)
                free[e] = ends[i] = max(ready[i], free[e]) + cyc[i]
                for j in post[i]:
                    ready[j] = max(ready[j], ends[i] + fly[j if back else i] + (0 if q[j] == e == "T" else WAKE))
                    left[j] -= 1
                    if not left[j]:
                        todo.append(j)
            return max(ends[i] + (0 if back else fly[i]) for i in range(n)), order, ends
        ends, best = [200.0 * i for i in range(n)], ORDER.get(n)
        for turn in range(0 if best else TURNS):
            rest = [x + y for x, y in zip(plan(post, pre, ends, True)[2], more)]
            now = plan(pre, post, [1e9 - 1e4 * i for i in range(2 * nld[0])] + rest[2 * nld[0]:], False)
            ends = now[2]
            best = min(best or now, now)
        ORDER[n] = best
        for i in best[1]:
            if what[i]:
                what[i]()

    def v(n, a=0, b=None, st=1, p=128):
        b = T[n].shape[1] if b is None else b
        return (T[n][0:p, a:b:st] if st > 1 else T[n][0:p, a:b], [(n, a, b)], (b - a + st - 1) // st)

    def v3(n, a, e, r=None):
        w = 16 * NV
        c, d = a // w, e // w
        if e - a <= w and r is None:
            return (T[n][:, c, 16 * (a % w):16 * (a % w + e - a)], [(n, a, e)], 16 * (e - a))
        return (T[n][:, c:d, :] if r is None else T[n][:, c:d, w * r:w * r + w], [(n, a, e)], (e - a) * (16 if r is None else 1))

    def ind(win, off):
        return (win[0].indirect(off[0]), win[1] + off[1], None)

    def cost(o, x, rate=None):
        if x[2] is None:
            return 70 + GATHER * o[2]
        if rate is None:
            rate = 0.5 if all(SCRATCH[y[1][0][0]][2].endswith("16") for y in (o, x)) else 1
        return max(64, rate * o[2])

    def tt(o, x, y, f):
        op("V", lambda: g.vector.tensor_tensor(o[0], x[0], y[0], f), x[1] + y[1], o[1], cost(o, x, 1 if bank(x[1][0][0]) or bank(y[1][0][0]) else 2))

    def ts(o, x, s1, f0, s2=None, f1=None):
        rd = x[1] + [r for c in (s1, s2) if isinstance(c, tuple) for r in c[1]]
        q1, q2 = [c[0] if isinstance(c, tuple) else c for c in (s1, s2)]
        if f1 is None:
            op("V", lambda: g.vector.tensor_scalar(o[0], x[0], q1, None, f0), rd, o[1], cost(o, x))
        else:
            op("V", lambda: g.vector.tensor_scalar(o[0], x[0], q1, q2, f0, f1), rd, o[1], cost(o, x))

    def cp(o, x, f=None):
        op("V", lambda: g.vector.tensor_copy(o[0], x[0]), x[1], o[1], cost(o, x))

    def turn(o, x):
        op("V", lambda: g.vector.transpose(o[0], x[0]), x[1], o[1], cost(o, x))

    def scan(o, x, f):
        s = v("seg", 0, o[2])
        op("V", lambda: g.vector.tensor_tensor_scan(o[0], s[0], x[0], 0.0, A.mult, f), s[1] + x[1], o[1], cost(o, x))

    def fill(o, c):
        op("V", lambda: g.vector.memset(o[0], c), [], o[1], cost(o, o))

    def act(o, x, f, bias=0.0, scale=1.0):
        rd = x[1] + [r for c in (bias, scale) if isinstance(c, tuple) for r in c[1]]
        bb, cc = [c[0] if isinstance(c, tuple) else c for c in (bias, scale)]
        op("S", lambda: g.scalar.activation(o[0], x[0], f, bias=bb, scale=cc), rd, o[1], cost(o, x, 1))

    def mm(prods, start=True, stop=True):
        def f():
            ins = None
            for j, (o, l, r) in enumerate(prods):
                ins = g.tensor.matmul(o[0], l[0], r[0], start and j == 0, stop and j == len(prods) - 1)
            return ins
        op("T", f, [x for o, l, r in prods for x in l[1] + r[1]], [x for o, l, r in prods for x in o[1]],
           sum(max(64, r[2]) * (2 if l[1][0][0] == "If" else 0.5) for o, l, r in prods))

    def iota(o, pattern, base, ch):
        op("G", lambda: g.iota(o[0], pattern, base, ch), [], o[1], 160 + 2 * o[2])

    def conv(o, x):
        op("G", lambda: g.affine_select(o[0], x[0], [[0, o[2]]], A.is_equal, 0.0, 0, 0), x[1], o[1], 200 + 2 * o[2])

    nld = [0, 0]

    def size(x):
        return 128 * x[2] * (2 if SCRATCH[x[1][0][0]][2].endswith("16") else 4)

    def load(o, src, e="Y"):
        s = "ld%d" % nld[0]
        nld[0] += 1
        op(e, lambda: ENG[e].dma_start(o[0], src), [], o[1], 100, s, None, size(o))

    def store(dst, src, e="Y"):
        s = "st%d" % nld[1]
        nld[1] += 1
        op(e, lambda: ENG[e].dma_start(dst, src[0]), src[1], [], 100, s, None, size(src))

    def move(dst, src, s, upto=None):
        op("Y", lambda: g.sync.dma_start(dst[0], src[0]), src[1], dst[1], 100, s, upto, size(src))

    def flat(j, plane):
        return (T.FLAT[plane:128:16, FW * j + 8:FW * j + FW], [("FLAT%d" % plane, j, j + 1)])

    load(v("skb"), T.sk[:])
    for n, src in enumerate((T.gs, T.gf, T.gcl)):
        for h in range(2):
            load(v("LT", 32 * n + 16 * h, 32 * n + 16 * h + 16), src[h:8:2, :], "YS"[h])
    load(v("frb"), T.fr[:])
    load(v("thi", 0, 1), T.th[:], "S")
    load(v("xr", 592, 8192), T.x[:, 0:7600])
    load(v("xr", 0, 592), T.x[:, 7600:8192])

    iota(v("it", 0, 128), [[-1, 128]], 0, 1)
    iota(v("it", 128, 256), [[-16, 8], [0, 16]], 0, 1)
    iota(v("il", 0, 32), [[16, 32]], 0, 0)
    iota(v("il", 32, 33), [[0, 1]], 0, 1)
    iota(v("it", 256, 384), [[16, 8], [128, 16]], -1016, 0)
    iota(v("CI"), [[1, 128]], 4096 + 512, 0)

    def window(j):
        return (T.FLAT[:, FW * j:FW * j + FW], [("FLAT%d" % q, j, j + 1) for q in range(6)], FW)
    for j in range(4):
        if ZERO[j] == "G":
            iota(window(j), [[0, FW]], 0, 0)
        elif ZERO[j] == "V":
            op("V", lambda j=j: g.vector.memset(window(j)[0], 0), [], window(j)[1], FW)
        else:
            op("Y", lambda j=j: g.sync.dma_start(window(j)[0], window(0)[0]), window(0)[1], window(j)[1], 100, "z%d" % j, None, 512 * FW)
    SCALES = (1.0, None, 2048.0, float(-(5 << 20)), float(-(13 << 20)), -1.0, float(-(1 << 23)), -592.0, -16.0, float(-(1 << 24)),
              -0.5, -8192.0, 1024.0, -592.0 * 1024)

    def put(o, x, pattern, c):
        op("G", lambda: g.affine_select(o[0], x[0], pattern, A.not_equal, c, 0, 1), x[1], o[1], 200 + 2 * o[2])

    def IM(c):
        j = SCALES.index(c)
        return v("Ib", 128 * j, 128 * j + 128)
    ONE, W16, BO = IM(1.0), IM(None), v("BO", 0, 128)
    ONES = v("row", 0, 512, 1, 1)

    def RC(j):
        return v("row", 512 + 128 * j, 640 + 128 * j, 1, 1)

    def Wq(j, q):
        return v("Vm", 144 * j + 15 - q, 144 * j + 143 - q)

    def BY(y):
        return v("BY", 128 * y, 128 * y + 128)
    ts(ONE, v("it", 0, 128), 0, A.is_equal)
    ts(v("it", 0, 128), v("it", 0, 128), 15, A.bitwise_and)
    ts(W16, v("it", 0, 128), 0, A.is_equal)
    ts(v("M16"), v("it", 0, 16), 0, A.is_equal)
    ts(v("it", 128, 256), v("it", 128, 256), 4, A.arith_shift_right)
    ts(BO, v("it", 128, 256), 0, A.is_equal)
    for c in SCALES[2:5]:
        act(IM(c), ONE, F.Copy, 0.0, c)
    act(v("If"), ONE, F.Copy)
    for y in range(16):
        act(BY(y), BO, F.Identity, 0.0, v("M16", y, y + 1))
    fill(v("row", 0, 512, 1, 1), 1.0)
    for j, c in enumerate((float(-(1 << 24)), float(1 << 24), 4096.0, -3072.0)):
        fill(RC(j), c)
    for j in range(2):
        c = (512 * j, 512 * j + 512)
        cp(v("skh", *c), v("skb", *c))
        act(v("skv", *c), v("skb", *c), F.Sign, -1023.5)
        mm([(v("pA%d" % j), IM(2048.0), v("skh", *c)), (v("pA%d" % j), IM(SCALES[3]), v("skv", *c))])
    act(v("T12", 0, 512), v("pA0"), F.Copy, float(C0 - 4096 + (7 << 20)))
    ts(v("T12", 512, 1024), v("pA1"), float(C0 - 4096 + (7 << 20)), A.add)
    cp(v("LF"), v("LT"))
    turn(v("LL"), v("LF"))
    cp(v("L0"), v("LL", 0, 64))
    cp(v("IH", 32, 64), v("LL", 32, 64))
    ts(v("lo"), v("frb"), -(1 << 31) + (1023 << 10), A.bitwise_and)
    ts(v("pK0"), v("frb"), float(C0 + (1 << 23)), A.add)
    tt(v("FB", 0, 512), v("lo"), v("pK0"), A.add)
    ts(v("CL"), v("LL", 64, 96), 1024.0, A.add)
    ts(v("il", 32, 33), v("il", 32, 33), 15, A.bitwise_and)
    cp(v("thf", 7, 8), v("il", 32, 33))
    ts(v("IH", 0, 32), v("il", 0, 32), v("thf", 7, 8), A.add)
    for j in range(2):
        c = (512 * j, 512 * j + 512)
        q = ("pM", "pN")[j]
        mm([(v(q), IM(2048.0), v("skh", *c)), (v(q), IM(SCALES[4]), v("skv", *c))])

    def tables_b():
        for j in range(2):
            act(v("T12", 1024 + 512 * j, 1536 + 512 * j), v(("pM", "pN")[j]), F.Copy, float(C0 - 4096 - (1 << 20)))

    def constants_v():
        fill(v("Vm", 0, 144), 0.0)
        cp(v("Vm", 15, 143, 16), v("BO", 0, 128, 16))
        cp(v("ST"), v("LL"))
        iota(v("oi", 0, 512, 1, 1), [[1, 512]], 512, 0)
        conv(v("cir", 0, 512, 1, 1), v("oi", 0, 512, 1, 1))
        ts(v("OF"), v("it", 256, 384), v("thf", 7, 8), A.add)
        fill(v("CW"), 0.0)
        fill(v("CW", 0, 1), float(-(1 << 25)))
        fill(v("seg"), 1.0)
        fill(v("seg", 0, 128, 16), 0.0)
        ts(v("thi", 1, 2), v("thi", 0, 1), 4, A.arith_shift_right)
        ts(v("thi", 2, 3), v("thi", 0, 1), 15, A.bitwise_and)
        ts(v("thi", 3, 4), v("thi", 0, 1), 1.0, A.add)
        ts(v("thi", 3, 4), v("thi", 3, 4), 1, A.arith_shift_right)
        cp(v("thf", 0, 3), v("thi", 1, 4))
        ts(v("H2"), v("it", 0, 128), 0.0, A.mult, v("thf", 2, 3), A.add)
        for j in range(4):
            move(flat(j, 4), v("H2"), "h2", 64)

    def constants_s():
        for c in SCALES[5:]:
            put(IM(c), ONE, [[-1, 128]], c)
        for j, c in ((1, -8192.0), (2, 4096.0), (3, -4096.0)):
            act(v("Vm", 144 * j, 144 * j + 144), v("Vm", 0, 144), F.Copy, 0.0, c)
        for j in range(4):
            act(v("Vm", 144 * (4 + j), 144 * (5 + j)), v("Vm", 0, 144), F.Identity, 0.0, v("M16", j, j + 1))
        act(v("Vm", 144 * 8, 144 * 9), v("Vm", 144 * 3, 144 * 4), F.Identity, 0.0, v("M16", 4, 5))
        for j in range(2):
            act(v("thf", 3 + j, 4 + j), v("M16", 2 * j, 2 * j + 1), F.Identity, v("M16", 2 * j + 1, 2 * j + 2), 1024.0)
            act(v("Vm", 144 * (9 + j), 144 * (10 + j)), v("Vm", 0, 144), F.Identity, 0.0, v("thf", 3 + j, 4 + j))
        for j in range(2):
            act(v("TH", 128 * j, 128 * j + 128), W16, F.Identity, 0.0, v("thf", j, j + 1))
        act(v("BO", 128, 256), BO, F.Copy, 0.0, 16.0)
        mm([(v("pK0", 0, 128), v("BO", 128, 256), v("TH", 0, 128)), (v("pK0", 0, 128), BO, v("TH", 128, 256))])
        act(v("TK"), v("pK0", 0, 128), F.Copy, -4096.0, -4096.0)
        act(v("B5"), BY(5), F.Copy, 0.0, float(1 << 24))
        iota(v("it", 384, 512), [[0, 128]], 1, 0)
        for j in range(4):
            move(flat(j, 5), v("it", 384, 512), "h3", 64)

    def spread(p, x, a=0, e=512):
        return [(v(p, a + y, e, 16), BY(y), v(x[0], x[1] + a // 16, x[1] + e // 16)) for y in range(16)]

    OWN = (0, 512, 1536)
    H0, H1 = (0, 256), (256, 512)
    PM = {p[0]: b for p, b in zip(MV, ("pM", "pC", "pM"))}
    PN = {p[0]: b for p, b in zip(MV, ("pN", "pK1", "pN"))}

    def lists(t, j, a, e):
        c, d = [p for p in (LP if t else ((0, 512),)) if p[0] <= a and e <= p[1]][0]
        o = (2 * c + j * (d - c) - c) // 16
        return v("L%d" % t, o + a // 16, o + e // 16)

    def came(t):
        return v("RW", 1024 * t - 1024, 1024 * t) if t else v("FB", 0, 512)

    def ghost(t, a, e):
        return v("FB", OWN[t] + 512 + a, OWN[t] + 512 + e) if t else v("Fg", a, e)

    def ab(t, a):
        return "pK1" if t and a >= 384 else "pA%d" % (a // 256)

    def goal_s(t, a, e):
        p = ab(t, a)
        mm([(v(p, a, e), RC(2), v("row", a, e, 1, 1))]
           + ([(v(p, a, e), v("row", 0, 128, 1, 1), v("cir", a, e, 1, 1))] if t else spread(p, ("IH", 32), a, e)), True, False)
        act(v("Ts", a, e), ind(v("T12", 0, 1024), lists(t, 0, a, e)), F.Copy)
        mm([(v(p, a, e), v("If"), v("Ts", a, e))], False, True)

    def goal_f(t, a, e):
        act(ghost(t, a, e), ind(came(t), lists(t, 1, a, e)), F.Copy)

    def clause_s():
        act(v("Tc"), ind(v("T12"), v("CL")), F.Copy)

    def clause_t(t):
        mm([(v("pC"), RC(2), ONES)] + spread("pC", ("nw", 96) if t else ("IH", 0)), True, False)
        mm([(v("pC"), v("If"), v("Tc"))], False, True)

    def offs(t, a, e, s, on_v):
        ts(v("P" + s, a, e), v("X" + s, a, e), 11, A.arith_shift_right, 2047, A.bitwise_and)
        ts(v("Q" + s, a, e), v("X" + s, a, e), 2047, A.bitwise_and)
        if on_v or s not in QP:
            tt(v("PR" + s, a, e), v("P" + s, a, e), v("Q" + s, a, e), A.mult)
        else:
            h, p = v("QH" if s == "G" else "QI", a, e), v("pK2" if s == "G" else "pK0", a, e)
            conv(h, v("Q" + s, a, e))
            mm([(p, ONE, h)])
            tt(v("PR" + s, a, e), v("P" + s, a, e), p, A.mult)
        c, d = a // (16 * NV), e // (16 * NV)
        ts((T["OI" + s][:, c:d, :], [("OI" + s, a, e)], e - a), v("PR" + s, a, e), 4, A.arith_shift_right, 8191, A.bitwise_and)
        for j in range(NV):
            (cp if on_v else conv)(v("O" + s, a + j, e, NV), (T["OI" + s][:, c:d, 16 * j:16 * j + 16], [("OI" + s, a, e)], (e - a) // NV))
        for j in range(a // 128, e // 128):
            for q, n in enumerate("PQ"):
                move(flat(j, q + 2 * (s == "C")), v(n + s, 128 * j, 128 * j + 128), "fl%d" % j, 64 * (t + 1))

    def goal(t, a, e, on_v=False):
        if t and a < DIRECT:
            tt(v("AG", a, e), ind(v("T12", 0, 1024), lists(t, 0, a, e)), v("CI", a, e), A.add)
            tt(v("XG", a, e), ind(came(t), lists(t, 1, a, e)), v("AG", a, e), A.max)
        else:
            tt(v("XG", a, e), ghost(t, a, e), v(ab(t, a), a, e), A.max)
        offs(t, a, e, "G", on_v)

    def clause_e(a, e):
        ts(v("EG", a, e), v("XG", a, e), (1 << 22) - 1, A.bitwise_and)

    def clause(t, a, e, on_v=False):
        if t == 0:
            tt(v("pC", a, e), v("EG", a, e), v("pC", a, e), A.max)
            tt(v("XC", a, e), v("FB", a, e), v("pC", a, e), A.max)
        else:
            tt(v("A2", a, e), v("EG", a, e), v("pC", a, e), A.max)
            tt(v("XC", a, e), ind(v("FB", OWN[t], OWN[t] + 1024), v("HL", a // 16, e // 16)), v("A2", a, e), A.max)
        offs(t, a, e, "C", on_v)

    def free_rows(a, e):
        act(v("sgf", a, e), v("XC", a, e), F.Sign, 0.5 - (1 << 22))

    def bind_prep(t):
        if t < 2:
            conv(v("EF"), v("EG"))
        else:
            conv(v("PH"), v("PG"))
            conv(v("QH"), v("QG"))
        bind_first(t, *MV[0])
        if t:
            keep_prep(*MV[0])

    def bind_first(t, a, e):
        p = v(PM[a], a, e)
        mm([(p, RC(0), v("row", a, e, 1, 1))] + ([(p, v("If"), v("EF", a, e))] if t < 2 else
           [(p, IM(2048.0), v("PH", a, e)), (p, ONE, v("QH", a, e)), (p, ONE, v("QH", a, e))]), True, False)

    def bind_free(a, e):
        mm([(v(PM[a], a, e), IM(float(-(1 << 23))), v("sgf", a, e))], False, False)

    def keep_prep(a, e, stop=False):
        p = v(PN[a], a, e)
        mm([(p, RC(1), v("row", a, e, 1, 1)), (p, IM(float(-(1 << 24))), v("mu", a, e))], True, stop)

    def kb(a, e):
        return v("pK%d" % (a // 128 % 3), a, e)

    def grec(a, e):
        act(v("U", 16 * a, 16 * e), ind(v("xr"), v("OG", a, e)), F.Copy)

    def th_first(j):
        p = kb(128 * j, 128 * j + 128)
        mm([(p, ONE, v("OF")), (p, RC(3), v("row", 0, 128, 1, 1))], True, False)

    def ksum(c, j, n):
        a, e = 64 * c, 64 * c + 64
        mm([(kb(a, e), Wq(j, r), v3(n, a, e, r)) for r in range(16)], False, c % 2 == 1 and j != 2)

    def crec_v(c):
        for a in range(64 * c, 64 * c + 64, 16 * NV):
            e = a + 16 * NV
            tt(v3("D3", a, e), ind(v("xr"), v("OC", a, e)), v("U", 16 * a, 16 * e), A.subtract)

    def abs_a(c):
        act(v3("R3", 64 * c, 64 * c + 64), v3("D3", 64 * c, 64 * c + 64), F.Abs)
        ksum(c, 3, "R3")

    def relu_v(c):
        ksum(c, 2, "D3")
        ts(v3("R3", 64 * c, 64 * c + 64), v3("D3", 64 * c, 64 * c + 64), 0.0, A.max)
        ksum(c, 1, "R3")

    def crec_s(t, c, m):
        p, w, u = v("pA%d" % m), 1024 * CS[t].index(c) + 512 * m, 1024 * c + 512 * m
        act(v("W2", w, w + 512), ind(v("xr"), v("OC", 64 * c + 32 * m, 64 * c + 32 * m + 32)), F.Copy)
        mm([(p, ONE, v("W2", w, w + 512)), (p, IM(-1.0), v("U", u, u + 512))])

    def abs_s(c, m):
        act(v3("D3", 64 * c + 32 * m, 64 * c + 32 * m + 32), v("pA%d" % m), F.Abs)

    def count(a, e):
        tt(v("sg", a, e), kb(a, e), v("TK"), A.is_ge)
        scan(v("Cn", a, e), v("sg", a, e), A.add)

    def best(a, e):
        tt(v("km", a, e), kb(a, e), v("sg", a, e), A.mult)
        scan(v("Mn", a, e), v("km", a, e), A.min)

    def clash(t, n, f, a, e):
        o, c = v(n, a // 16, e // 16), v("Cn", a + 15, e, 16)
        if t:
            tt(o, c, v("av", a // 16, e // 16), f)
        else:
            ts(o, c, 9.0, f)

    def pick(t, a, e, by):
        c = (a // 16, e // 16)
        tt(v("kf", *c), v("Mn", a + 15, e, 16), v("ncl", *c), A.mult)
        ts(v("ko", *c), v("kf", *c), 4095, A.bitwise_and)
        cp(v("ML", *c), v("ko", *c))
        for j in range(a // 128, e // 128):
            by(v("res", 128 * j, 128 * j + 128), ind(window(j), v("ML", 8 * j, 8 * j + 8)), F.Copy)

    def lsum(p, o, plane, a=0, e=512):
        return [(v(p, o, o + (e - a) // 16), Wq(4 + plane, q), v("res", a + q, e, 16)) for q in range(16)]

    def chosen(p, o, plane, a=0, e=512):
        c, d, out = a // 16, e // 16, v(p, o, o + (e - a) // 16)
        mm(lsum(p, o, plane, a, e) + [(out, IM(-16.0 if plane % 2 else -592.0), v("ncl", c, d)),
                                      (out, ONE, v("Zc", 32 * plane + c, 32 * plane + d))])

    def on_clash(plane, a=0, e=512):
        x, o = (("ST", 0), ("ST", 32), ("NX", 0), ("IH", 0))[plane]
        tt(v("Zc", 32 * plane + a // 16, 32 * plane + e // 16), v(x, o + a // 16, o + e // 16), v("cl", a // 16, e // 16), A.mult)

    def goals_out(t, a, e):
        c, n, b = a // 16, (e - a) // 16, LP.index((a, e))
        for plane in range(2):
            on_clash(plane, a, e)
            chosen("pK2", plane * n, plane, a, e)
        cp(v("LS", 2 * c, 2 * c + 2 * n), v("pK2", 0, 2 * n))
        send(t, v("L%d" % (t + 1), 2 * c, 2 * c + 2 * n), v("LS", 2 * c, 2 * c + 2 * n), "as%d%d" % (t, b), "ls%d%d" % (t, b))
        for plane in range(2):
            act(v("nw", 32 * plane + c, 32 * plane + c + n), v("pK2", plane * n, plane * n + n), F.Copy)

    def own_last(t, a, e):
        p, f = v(PM[a], a, e), v("FB", OWN[t] + a, OWN[t] + e)
        mm([(p, v("If"), v("EF", a, e)), (p, IM(float(-(1 << 23))), v("sgf", a, e))])
        tt(v("A2", a, e), f, p, A.max)
        if t:
            keep_prep(a, e, True)
            tt(v("keep", a, e), f, v(PN[a], a, e), A.min)
            cp(v("NU", a // 16, e // 16), v("ncl", a // 16, e // 16))
        else:
            ts(v("NU", a // 16, e // 16), v("Cn", a + 15, e, 16), 9.0, A.is_ge)
        tt(v("Ts", a, e), ind(v("CW"), v("NU", a // 16, e // 16)), v("A2", a, e), A.add)
        o = v("FB", OWN[t + 1] + a, OWN[t + 1] + e)
        tt(o, v("Ts", a, e), v("keep", a, e) if t else f, A.max)
        b = MV.index((a, e))
        send(t, v("RW", 1024 * t + a, 1024 * t + e), o, "ac%d%d" % (t, b), "lc%d%d" % (t, b))

    def own_mm(t, a, e):
        if a:
            bind_first(t, a, e)
            bind_free(a, e)
        if t:
            if a:
                keep_prep(a, e)
            mm([(v(PN[a], a, e), v("B5"), v("res", a, e))], False, True)
        mm([(v(PM[a], a, e), v("B5"), v("res", a, e))], False, True)

    def own_new(t, a, e):
        if t:
            tt(v("keep", a, e), v("FB", OWN[t] + a, OWN[t] + e) if t < 2 else v("yv", a, e), v(PN[a], a, e), A.min)
        o = v("FB", OWN[t + 1] + a, OWN[t + 1] + e) if t < 2 else v("yv", a, e)
        tt(o, v("keep", a, e) if t else v("FB", a, e), v(PM[a], a, e), A.max)
        if t < 2:
            b = MV.index((a, e))
            send(t, v("RW", 1024 * t + a, 1024 * t + e), o, "ac%d%d" % (t, b), "lc%d%d" % (t, b))
        else:
            ts(o, o, float(-(C0 + 16 + (1 << 23))), A.add, -1.0, A.max)

    def next_clash():
        ts(v("n1"), v("ST", 0, 32), 32.0, A.add)
        tt(v("n2"), v("n1"), v("ST", 64, 96), A.mult)
        ts(v("n2"), v("n2"), 32.0, A.add)
        ts(v("NX"), v("n2"), 5, A.arith_shift_right, 1023, A.bitwise_and)

    def half_th():
        mm(lsum("pK1", 96, 4) + [(v("pK1", 96, 128), IM(float(-(1 << 24))), v("cl"))])
        tt(v("ncs"), v("Mn", 15, 512, 16), v("pK1", 96, 128), A.is_lt)

    def clause_lists():
        tt(v("eq"), v("nw", 96, 128), v("IH", 0, 32), A.is_equal)
        mm([(v("pM", 32, 64), ONE, v("nw", 64, 96)), (v("pM", 32, 64), IM(1024.0), v("eq"))])
        cp(v("HL"), v("pK0", 32, 64))
        cp(v("CL"), v("pM", 32, 64))

    def saves():
        p = v("pK1", 0, 96)
        mm([(p, RC(2), v("row", 0, 96, 1, 1)), (p, ONE, v("nw", 0, 96))]
           + [(v("pK1", 32 * j, 32 * j + 32), IM(-8192.0), v("ncs")) for j in range(3)])

    def saved():
        tt(v("SI"), v("ST"), v("pK1", 0, 96), A.max)
        ts(v("ST"), v("SI"), 4095, A.bitwise_and)

    def marks(t):
        b = "pN" if t < 2 else "pC"
        mm([(v(b), IM(-0.5), v("sgf"))] + ([(v(b), ONE, v("mu"))] if t else []), True, False)
        mm(spread(b, ("ncs", 0)), False, True)
        for h in ((0, 512),) if t < 2 else (H0, H1):
            act(v("mu" if t < 2 else "pK2" if h[0] else "pK0", *h), v(b, *h), F.Relu, -0.5)

    def parity_mm():
        mm([(v("pM", 0, 32), W16, v("cl"))])

    def parity():
        cp(v("ai"), v("pM", 0, 32))
        ts(v("ai"), v("ai"), 1, A.bitwise_and)
        ts(v("av"), v("ai"), -1.0, A.mult, 9.0, A.add)

    def send(t, dst_view, src_view, rs, ls):
        calls.append(("G", lambda: send_now(t, dst_view, src_view, rs, ls), src_view[1], dst_view[1],
                      4000 if rs == "ag0" else 600, FAR * size(src_view), soon[0]))

    def send_now(t, dst_view, src_view, rs, ls):
        dst = T.cores[(rank + t + 1) % len(T.cores)]
        rid, pid, _ = topo.addr(dst)
        k = len(topo.engines(core, dst))
        touch("G", src_view[1], [])
        g.remote_dma(dst_view[0], src_view[0], T.sem[rs], T.sem[ls], pid, rid, topo.mask(core, dst))
        cnt[ls] = k
        note(ls, (ls, k, dict(known["G"])), src_view[1], [])
        src = T.cores[(rank - t - 1) % len(T.cores)]
        cnt[rs] = len(topo.engines(src, core))
        note(rs, (rs, cnt[rs], {}), [], dst_view[1])

    def packed(b, plane):
        p = v(b, 0, 32)
        mm([(p, Wq(9 + plane // 2, q), v("res", q, 512, 16)) for q in range(16)]
           + [(p, IM(-592.0 * 1024), v("ncl")), (p, IM(-16.0), v("ncl")), (p, IM(1024.0), v("Zc", 32 * plane, 32 * plane + 32)),
              (p, ONE, v("Zc", 32 * plane + 32, 32 * plane + 64))])

    def frames_old():
        for a, e in MV:
            conv(v("oi", a, e), v("FB", OWN[2] + a, OWN[2] + e))
            ts(v("lo", a, e), v("oi", a, e), 2047, A.bitwise_and)
            tt(v("yv", a, e), v("oi", a, e), v("lo", a, e), A.add)
        ts(v("LF", 0, 32), v("ST", 0, 32), 1024.0, A.mult)
        cp(v("LF", 32, 64), v("ST", 64, 96))
        tt(v("LF", 0, 32), v("LF", 0, 32), v("ST", 32, 64), A.add)

    for t in range(3):
        if t == 0:
            goal_s(t, *H0)
            goal_f(t, *H0)
            tables_b()
            clause_s()
            clause_t(t)
        else:
            goal_s(t, DIRECT, 256)
            goal_f(t, *H0)
        for p in (H1,) if t == 0 else ((256, 384), (384, 512)):
            goal_s(t, *p)
            goal_f(t, *p)
        if t == 0:
            constants_v()
            constants_s()
            next_clash()
        for a, e in GP:
            goal(t, a, e, a == 0 or (t == 0 and a < ON_V))
        for h in (H0, H1):
            clause_e(*h)
            clause(t, *h, t == 0 and h[0] < ON_C)
        for p in UP:
            grec(*p)
        if t < 2:
            send(t, v("RW", 1024 * t + 512, 1024 * t + 1024), v("FB", 1024 * t, 1024 * t + 512), "ag%d" % t, "lg%d" % t)
        soon[0] = SOON[0]
        bind_prep(t)
        free_rows(0, 512)
        bind_free(*MV[0])
        soon[0] = 0
        if t == 2:
            frames_old()
        for j in range(4):
            th_first(j)
            for c in (2 * j, 2 * j + 1):
                if c in CS[t]:
                    for m in range(2):
                        crec_s(t, c, m)
                        abs_s(c, m)
                    ksum(c, 3, "D3")
                else:
                    crec_v(c)
                    (abs_a if c in CA[t] else relu_v)(c)
            soon[0] = SOON[1]
            count(128 * j, 128 * j + 128)
            best(128 * j, 128 * j + 128)
            soon[0] = 0
        soon[0] = SOON[2]
        for b, p in enumerate(MV):
            clash(t, "ncl", A.is_ge, *p)
            pick(t, *p, act if RES[b] else cp)
            if t < 2 and p[1] == 512 and LAST:
                own_last(t, *p)
            else:
                own_mm(t, *p)
                own_new(t, *p)
        if t == 2:
            clash(t, "cl", A.is_lt, 0, 512)
            for plane in range(4):
                on_clash(plane)
            break
        for p in LP:
            clash(t, "cl", A.is_lt, *p)
            goals_out(t, *p)
        soon[0] = SOON[3]
        on_clash(2)
        on_clash(3)
        chosen("pK0", 0, 2)
        chosen("pK0", 32, 3)
        parity_mm()
        parity()
        act(v("nw", 64, 128), v("pK0", 0, 64), F.Copy)
        half_th()
        clause_lists()
        saves()
        marks(t)
        clause_s()
        clause_t(t + 1)
        saved()
        next_clash()
        soon[0] = 0
    soon[0] = 0
    half_th()
    marks(2)
    packed("pA0", 0)
    chosen("pA0", 32, 2)
    packed("pA1", 2)
    for a, e in (H0, H1):
        tt(v("yr", a, e), v("yv", a, e), v("pK2" if a else "pK0", a, e), A.add)
        store(T.yf[:, a:e], v("yr", a, e), "YS"[a > 0])
    d = v("LL", 0, 64)
    tt(d, v("pA0", 0, 64), v("LF", 0, 64), A.subtract)
    turn(v("OUT", 32, 64), v("pA0", 0, 32))
    turn(v("OUT", 0, 32), v("pA1", 0, 32))
    for j in range(2):
        tt(v("LL", 32 * j, 32 * j + 32), v("LL", 32 * j, 32 * j + 32), v("ncs"), A.mult)
    tt(d, v("pA0", 0, 64), d, A.subtract)
    turn(v("OUT", 64, 128), d)
    for j, y in enumerate((T.yc, T.yg, T.ysg, T.yk)):
        for h in range(2):
            store(y[h:8:2, :], v("OUT", 32 * j + 16 * h, 32 * j + 16 * h + 16), "YS"[h])
    issue_all()
    for s in cnt:
        g.wait_ge(T.sem[s], cnt[s])
